import numpy as np, ml_dtypes
CORES = [10,34,74,98]
N = 4
import mx_ref
BF = ml_dtypes.bfloat16
def gentries(a):
    return np.ascontiguousarray(a.reshape(8, 16, -1).transpose(0, 2, 1)).reshape(8, -1)
def gtable(e):
    e = np.asarray(e); return np.ascontiguousarray(e.reshape(8, -1, 16).transpose(0, 2, 1)).reshape(128, -1).astype(np.int32)
def gcols(t, e):
    v = np.concatenate([t.reshape(8, 16, -1, 4), np.zeros((8, 16, 1, 4), BF)], axis=2)
    return np.ascontiguousarray(np.stack([v[g][:, e[g]] for g in range(8)])).reshape(128, -1)
def tile(rs):
    return np.stack(rs, axis=2).reshape(128, -1).astype(BF)
def pick(q, e):
    c = np.concatenate([q[0].reshape(128, -1, 4), np.zeros((128, 1, 4), np.uint8)], axis=1); s = np.concatenate([q[1], np.ones((16, 1), np.uint8)], axis=1)
    return (np.ascontiguousarray(c[:, e].reshape(128, -1)), np.ascontiguousarray(s[:, e]))
def join(*qs):
    return (np.concatenate([q[0] for q in qs], axis=1), np.concatenate([q[1] for q in qs], axis=1))
def put(q, e, v):
    c, s = q[0].reshape(128, -1, 4).copy(), q[1].copy(); c[:, e] = v[0].reshape(128, -1, 4); s[:, e] = v[1]
    return (c.reshape(128, -1), s)
def pk(c, s):
    return (np.ascontiguousarray(c), mx_ref.live(s))
def emit(q):
    return q[0], q[1]
def packed(v, rng):
    q = [mx_ref.quantize(np.ascontiguousarray(v[r])) for r in range(N)]
    return np.stack([a for a, b in q]), np.stack([mx_ref.plane(b, rng) for a, b in q])
def values_of_codes():
    e, c = np.zeros((128, 128, 4), np.float32), np.zeros((128, 2, 4), np.uint8)
    e[np.arange(128), np.arange(128), 0] = 1
    c[:127, :, 0] = np.arange(256).reshape(2, 128).T[:127]
    return mx_ref.matmul(mx_ref.quantize(e.reshape(128, 512).astype(BF)), (c.reshape(128, 8), np.full((16, 2), 127, np.uint8))).T.reshape(-1).astype(np.float64)
CODE_VALUE, SCALE_VALUE = values_of_codes(), 2.0 ** (np.arange(256) - 127.0)
def decode(q):
    return (CODE_VALUE[q[0]].reshape(16, 8, -1, 4) * SCALE_VALUE[q[1]][:, None, :, None] + 0.0).reshape(128, -1).astype(np.float32)
def f(rng, *shape):
    return mx_ref.flush((rng.standard_normal(shape, dtype=np.float32) * np.exp2(rng.integers(-2, 3, shape[:-1] + (1,)))).astype(BF))
def wide(rng, *shape, cols=0):
    v = rng.standard_normal(shape, dtype=np.float32) * np.exp2(rng.integers(-12, 13, shape)).astype(np.float32)
    if cols: v *= np.repeat(np.exp2(rng.integers(-cols, cols + 1, shape[:-2] + (1, shape[-1] // 4))) * (rng.random(shape[:-2] + (1, shape[-1] // 4)) > 0.0625), 4, axis=-1).astype(np.float32)
    return mx_ref.flush(v.astype(BF))
C = 448
STEP = [1, 2, 3]
def big(v):
    v = v.astype(np.float32)
    v[np.abs(v) < np.float32(2.0 ** -16)] = 0
    return v.astype(BF)
def numbers_of(rng):
    return {"x": big(f(rng, N, 128, 4 * C)), "u": np.array(f(rng, N, 128, 512)), "v": np.array(f(rng, N, 128, 512))}
def stored(k, t):
    return {"gl": np.stack([gtable(k[r]) for r in range(N)]), "ht": np.stack([gtable(t[r]) for r in range(N)])}
def lists(rng):
    e = np.tile(np.arange(C), (N, 8, 1))
    k = np.stack([rng.permuted(e, axis=2), rng.permuted(e, axis=2)], axis=3).reshape(N, 8, 2 * C)
    return stored(k, rng.integers(0, C, (N, 8, C)))
def layers(rng):
    return big(f(rng, N, 128, 2048)).reshape(N, 8, 16, 4, 8, 16, 4)
def weights(rng, w):
    c, p = packed(np.ascontiguousarray(w).reshape(N, 128, 2048), rng)
    return {"wc": c, "ws": p}
def setup_inputs(rng):
    return {**numbers_of(rng), **lists(rng), **weights(rng, layers(rng))}
def setup_inputs_ties(rng):
    d = numbers_of(rng)
    o = rng.permutation(N)
    k = rng.integers(-1, 2, (N, 8, C)).astype(np.float32)
    k[o[1]] = 1
    x = d["x"].reshape(N, 8, 16, C, 4)
    x[:, :, 0] = 0
    x[:, :, 0, :, 0] = k.astype(BF)
    c = np.ones(N, np.float32)
    c[o[0]] = 0
    c[o[2]] = -1
    u = d["u"].reshape(N, 128, 128, 4)
    u[:, :, ::16] = 0
    for h in range(0, 128, 16): u[:, h, h, 0] = c.astype(BF)
    w = layers(rng)
    w[:, :, :, :, :, :8] = 0
    return {"x": x.reshape(N, 128, 4 * C), "u": u.reshape(N, 128, 512), "v": d["v"], **lists(rng), **weights(rng, w)}
def setup_inputs_near(rng):
    d = numbers_of(rng)
    o = rng.permutation(N) % 2
    k = np.where(o == 0, 2.0 ** -30, 1.0).astype(np.float32)
    x = np.zeros((N, 8, 16, C, 4), np.float32)
    s = rng.integers(-1, 2, (N, 8, C)) * k[:, None, None]
    x[:, :, 0, :, 0] = 1.125 * s
    x[:, :, 1, :, 0] = -1.25 * s
    for r in range(N):
        for g in rng.permutation(8)[:4]: x[r, g, 0, rng.integers(C), 0] = 2.0 ** 30 * rng.choice([-1.0, 1.0])
    i = np.arange(N)
    e = ((i ^ (i >> 1) ^ (i >> 2))[:, None] + rng.permutation(8)) % 2
    a = (1 + (2 * rng.integers(0, 64, (N, 8, 8, C, 4)) + 1) * 2.0 ** -7) * np.exp2(12.0 - rng.integers(8, 15, (N, 8, 8, C, 4)))
    a[:, :, 0, :, 0] = -1.96875 * 2.0 ** 12
    a = np.where(e[:, :, None, None, None] == 0, -2.0 ** 26, a)
    x[:, :, 8:] = np.where(rng.random((N, 8, 1, C, 1)) < 0.5, a, 0.0)
    u = d["u"].reshape(N, 128, 128, 4)
    u[:, :, ::16] = 0
    for h in range(0, 128, 16):
        u[:, h, h, 0] = (1.125 * k).astype(BF)
        u[:, h + 1, h, 0] = k.astype(BF)
    w = layers(rng)
    w[:, :, :8] = 0
    w[:, :, :, :, :, :8] = 0
    return {"x": x.reshape(N, 128, 4 * C).astype(BF), "u": u.reshape(N, 128, 512), "v": d["v"], **lists(rng), **weights(rng, w)}
def setup_inputs_late(rng):
    d = numbers_of(rng)
    c = (rng.permutation(N) % 2 * 2.0 - 1.0).astype(np.float32).astype(BF)
    x = d["x"].reshape(N, 8, 16, C, 4)
    x[:, :, 0] = c[:, None, None, None]
    u = d["u"].reshape(N, 128, 128, 4)
    u[:, :, ::16] = 0
    for h in range(0, 128, 16): u[:, h, h, 0] = 1
    w = layers(rng)
    w[:, :, :, :, :, 0] = (w[:, :, :, :, :, 0].astype(np.float32) * 4).astype(BF)
    return {"x": x.reshape(N, 128, 4 * C), "u": u.reshape(N, 128, 512), "v": d["v"], **lists(rng), **weights(rng, w)}
def setup_inputs_ends(rng):
    d = numbers_of(rng)
    o, e = rng.permutation(N) % 4, rng.permutation(N) % 4
    s = rng.choice([-1.0, 1.0], (N, 128, C, 4))
    s[o == 0] = -1
    s[o == 1] = rng.choice([-1.0, 1.0], (N, 1, C, 1))[o == 1]
    x = s * (0.955 + 0.02 * rng.random((N, 128, C, 4))) * 2.0 ** 30
    x[:, :8] = 0
    x[:, 13] = -240 * 2.0 ** 22
    x[:, 14] = -249 * 2.0 ** 22
    x[:, 15] = 0
    x[o == 3] = 2.0 ** -30
    size = np.where(o == 3, 2.0 ** -30, 2.0 ** 30)
    a = np.stack([rng.permutation(8) % 2 * 2.0 - 1.0 for r in range(N)]) * size[:, None]
    u = d["u"].reshape(N, 128, 128, 4)
    u[:, :, ::16] = a.astype(np.float32).astype(BF)[:, None, :, None]
    v = rng.choice([-1.0, 1.0], (N, 128, 512)) * size[:, None, None]
    t = rng.integers(0, C, (N, 8, C))
    t[o == 0] = C - 1
    t[o == 1] = 0
    t[o == 2] = rng.integers(0, 2, (8, C)) * (C - 1)
    k = rng.integers(0, C, (N, 8, 2 * C))
    k[e == 0] = C - 1
    k[e == 1] = 0
    k[e == 1, 7] = C - 1
    k[e == 2] = np.arange(2 * C) % 2 * (C - 1)
    w = np.zeros((N, 128, 4, 128, 4), np.float32)
    i = np.arange(128)
    for b in range(4):
        w[:, i, b, i, b] = np.where(o == 3, 16.0, -0.25)[:, None]
        for r in range(N):
            if o[r] < 3:
                w[r, :8, b, :8, b] = 64 * np.eye(8)
                w[r, 13:16, b, 13:16, b] = [[0, 0, -64], [0, 0, 64], [0, 0, 0]]
    return {"x": x.astype(np.float32).reshape(N, 128, 4 * C).astype(BF), "u": u.reshape(N, 128, 512), "v": v.astype(np.float32).astype(BF), **stored(k, t), **weights(rng, w.astype(BF))}
def setup_inputs_spread(rng):
    d = setup_inputs(rng)
    d["x"] = big(wide(rng, N, 128, 4 * C, cols=6))
    return d
def check_inputs(d):
    b = []
    for k in ("x", "u", "v"):
        a = np.abs(d[k].astype(np.float32))
        if not (np.isfinite(a).all() and ((a == 0) | (a >= 2.0 ** -30) & (a <= 2.0 ** 30)).all()): b.append("a value of " + k)
    for k in ("gl", "ht"):
        if not ((d[k] >= 0) & (d[k] < C)).all(): b.append("an entry of " + k)
    none, least, most = [emit(mx_ref.quantize(np.full((128, 16), k, np.float32).astype(BF)))[1][0, 0] for k in (0.0, 2.0 ** -30, 2.0 ** 30)]
    for r in range(N):
        if ((d["wc"][r] == 0x7F) | (d["wc"][r] == 0xFF)).any(): b.append("wc: a code that is no number")
        s = mx_ref.live(d["ws"][r])
        if ((s != none) & ((s < least) | (s > most))).any(): b.append("ws: a scale out of range")
        if (((d["wc"][r].reshape(16, 8, 512, 4) & 0x7F) != 0) & (s == none)[:, None, :, None]).any(): b.append("wc: a code other than zero under the scale of zeros")
    return b
def reference(x, u, v, gl, ht, wc, ws):
    qu = [mx_ref.quantize(u[r]) for r in range(N)]
    lay = [pk(wc[r], ws[r]) for r in range(N)]
    guest, host = [gentries(gl[r]) for r in range(N)], [gentries(ht[r]) for r in range(N)]
    now = [x[r] for r in range(N)]
    y, pl = np.zeros((N, 128, C), np.float32), np.zeros((N, 8, C), np.float32)
    for step in STEP:
        q = [mx_ref.quantize(now[r]) for r in range(N)]
        bit = [(mx_ref.matmul(qu[r], q[r])[::16] > 0).astype(np.int64) for r in range(N)]
        made = []
        for r in range(N):
            p = r ^ step
            at, there = np.zeros((9, C), np.int64), np.zeros((8, C), np.int64)
            at[0] = np.arange(C)
            for g in range(8):
                there[g] = host[p][g][at[g]]
                at[g + 1] = guest[r][g][2 * at[g] + bit[p][g][there[g]]]
            far = gcols(decode(q[p]).astype(BF), there)
            z = mx_ref.quantize(np.maximum(gcols(now[r], at[:8]).astype(np.float32), far.astype(np.float32)).astype(BF))
            made.append(tile([mx_ref.matmul(pick(lay[r], np.arange(128 * b, 128 * b + 128)), z) * np.float32(0.015625) + now[r][:, b::4].astype(np.float32) for b in range(4)]))
            pl[r] = at[1:]
        now = made
    oc, osc = np.zeros((N, 128, 4 * C), np.uint8), np.zeros((N, 16, C), np.uint8)
    for r in range(N):
        q = mx_ref.quantize(now[r])
        y[r] = mx_ref.matmul(mx_ref.quantize(v[r]), q)
        oc[r], osc[r] = emit(q)
    return {"y": y, "pl": pl, "oc": oc, "osc": osc}

@@ -1,0 +1,489 @@
+from concourse.bass import DstId, RemoteDMATransfer
+from concourse.mybir import dt, AluOpType, ActivationFunctionType
+
+C = 448
+STEPS = (1, 2, 3)
+CHH = ((0, 224), (224, 448))
+CHZ = ((0, 160), (160, 320), (320, 448))
+CHL = ((0, 320), (320, 448))
+PIECE = 112
+BIG = 524288.0
+ALU = AluOpType
+COPY = ActivationFunctionType.Copy
+F8, U8, BF, F32, I32, U16 = "float8_e4m3fn_x4", "uint8", "bfloat16", "float32", "int32", "uint16"
+
+SCRATCH = {"pa": ("psum", [128, 2048], F32), "pb": ("psum", [128, 2048], F32)}
+
+
+def _sbuf(kind, **widths):
+    for name in widths:
+        SCRATCH[name] = ("sbuf", [128, widths[name]], kind)
+
+
+_sbuf(I32, gli=56, hti=28, uli=16, pi=1, lo=1, hi=1, idl=28, t1=448, n1=448)
+_sbuf(U16, gs=112, hx=56, hl=112, ul=16, l1=28, l2=28, l3=28, l8=28, r8=28)
+_sbuf(BF, ut=512, vt=512, ec=2048, eye=128, x64=1792)
+_sbuf(F8, qu=128, qp=256, qv=128, qe=512, qw=512)
+_sbuf(U8, qus=128, qps=256, qvs=128, qes=512, qws=512)
+_sbuf(F32, wt=96, tg=128, tg2=128, th=64, th2=64, lof=1, off=1, m16=16, da=16, db=16, dc=16, dd=16, de=16, d=448, gw=448,
+      wb=1792, b1=448, b2=448, t2=448, s2=448, s3=448, s4=448, o5=448, s5=448, lf=28, na0=896, nb0=896, na1=896, nb1=896,
+      tmp=1792, o8=448, s8=448, p7=448, p8=448, yb=448)
+for _k in range(4):
+    SCRATCH["x%d" % _k] = ("sbuf", [128, 1792], BF)
+    SCRATCH["qx%d" % _k] = ("sbuf", [128, 448], F8)
+    SCRATCH["qxs%d" % _k] = ("sbuf", [128, 448], U8)
+for _k in STEPS:
+    for _n, _w, _d in (("h", 1792, BF), ("m", 1792, BF), ("z", 1792, BF), ("qh", 448, F8), ("hc", 448, F8), ("qz", 448, F8),
+                       ("qhs", 448, U8), ("hcs", 448, U8), ("qzs", 448, U8), ("vl", 28, U16), ("vr", 28, U16), ("gr", 112, U16),
+                       ("ea", 448, F32), ("eb", 448, F32)):
+        SCRATCH["%s%d" % (_n, _k)] = ("sbuf", [128, _w], _d)
+SEMAPHORES = ["v", "s", "t", "p", "rl", "k8", "dgl", "dht", "dx0", "dx1", "du", "dw", "dv", "oo", "os_", "oy", "op_"]
+for _k in STEPS:
+    SEMAPHORES += ["g%d" % _k, "k%d" % _k, "c%da" % _k, "c%db" % _k]
+
+
+def rank_program(g, core, T, topo):
+    rank = T.rank_of(core)
+    if rank is None:
+        return
+    queue = {"v": g.vector, "s": g.scalar, "t": g.tensor, "p": g, "y": g.sync}
+    total, log = {}, {}
+    seen = dict((q, {}) for q in queue)
+
+    def A(name, a=0, b=None, step=1, p=None, cast=None, by=None):
+        t = T[name]
+        b = t.shape[1] if b is None else b
+        lo, hi = p if p else (0, 128)
+        reg = [(name, lo, hi, a, b, step)]
+        if name in ("pa", "pb"):
+            reg = [(name, 0, 128, a // 512 * 512, (b + 511) // 512 * 512, 1)]
+        if p:
+            v = t[lo:hi, a:b:step] if step > 1 else t[lo:hi, a:b]
+        else:
+            v = t[:, a:b:step] if step > 1 else t[:, a:b]
+        if cast is not None:
+            v = v.bitcast(cast)
+        if by is not None:
+            v = v.indirect(by[0])
+            reg = reg + by[1]
+        return v, reg
+
+    def touch(r, s):
+        apart = r[5] == s[5] and (r[3] - s[3]) % r[5] != 0
+        return r[1] < s[2] and s[1] < r[2] and r[3] < s[4] and s[3] < r[4] and not apart
+
+    def covers(r, s):
+        same = r[5] == 1 or r[5] == s[5] and (r[3] - s[3]) % r[5] == 0
+        return r[1] <= s[1] and s[2] <= r[2] and r[3] <= s[3] and s[4] <= r[4] and same
+
+    def waits(q, reads, writes):
+        need = {}
+        for regs, wr in ((reads, False), (writes, True)):
+            for r in regs:
+                for reg, was, sem, val in log.get(r[0], []):
+                    if touch(r, reg) and (wr or was or r[0] in ("pa", "pb")):
+                        need[sem] = max(need.get(sem, 0), total[sem] if val is None else val)
+        for sem in sorted(need):
+            if seen[q].get(sem, 0) < need[sem]:
+                queue[q].wait_ge(T.sem[sem], need[sem])
+                seen[q][sem] = need[sem]
+
+    def note(reads, writes, sem, val):
+        for r in writes:
+            log[r[0]] = [e for e in log.get(r[0], []) if not covers(r, e[0])] + [(r, True, sem, val)]
+        for r in reads:
+            log.setdefault(r[0], []).append((r, False, sem, val))
+
+    def run(q, call, outs, ins):
+        reads = [r for o in ins for r in o[1]]
+        writes = [r for o in outs for r in o[1]]
+        waits(q, reads, writes)
+        call().then_inc(T.sem[q], 1)
+        total[q] = total.get(q, 0) + 1
+        note(reads, writes, q, total[q])
+
+    def dma(q, out, in_, sem):
+        waits(q, in_[1], out[1])
+        queue[q].dma_start(out[0], in_[0]).then_inc(T.sem[sem], 16)
+        total[sem] = total.get(sem, 0) + 16
+        note(in_[1], out[1], sem, None)
+
+    def ext(view):
+        return view, []
+
+    def core_of(step):
+        return T.cores[rank ^ step]
+
+    def send(step, out, in_, sem):
+        dst = core_of(step)
+        waits("p", in_[1], [])
+        rid, pid, _ = topo.addr(dst)
+        g.remote_dma(out[0], in_[0], T.sem[sem], T.sem.rl, pid, rid, topo.mask(core, dst))
+        total["rl"] = total.get("rl", 0) + len(topo.engines(core, dst))
+
+    def send_both():
+        mv = []
+        waits("p", A("gs")[1], [])
+        for j, st in enumerate((2, 3)):
+            dst = core_of(st)
+            rid, pid, _ = topo.addr(dst)
+            eng = topo.engines(core, dst)
+            mine = eng[len(eng) // 2 * j:len(eng) // 2 * (j + 1)]
+            mv.append(RemoteDMATransfer(dst_ids=[DstId(rid=rid, pnc=pid)], dma_engine_mask=sum(1 << e for e in mine),
+                                        remote_sem=T.sem["g%d" % st], src=T.gs[:, :], dst=T["gr%d" % st][:, :]))
+            total["rl"] = total.get("rl", 0) + len(mine)
+        g.remote_dma_fused(mv, local_sem=T.sem.rl)
+
+    def arrives(step, out, sem, part=1):
+        total[sem] = total.get(sem, 0) + len(topo.engines(core_of(step), core)) // part
+        note([], out[1], sem, None)
+
+    def copy(out, in_, q="v"):
+        if q == "v":
+            run("v", lambda: g.vector.tensor_copy(out[0], in_[0]), [out], [in_])
+        else:
+            run("s", lambda: g.scalar.activation(out[0], in_[0], COPY), [out], [in_])
+
+    def scaled(out, in_, c):
+        run("s", lambda: g.scalar.activation(out[0], in_[0], COPY, scale=c), [out], [in_])
+
+    def ts(out, in_, a, op0, b=None, op1=None):
+        col = [a] if isinstance(a, tuple) else []
+        a0 = a[0] if col else a
+        if op1 is None:
+            run("v", lambda: g.vector.tensor_scalar(out[0], in_[0], a0, None, op0), [out], [in_] + col)
+        else:
+            run("v", lambda: g.vector.tensor_scalar(out[0], in_[0], a0, b, op0, op1), [out], [in_] + col)
+
+    def tt(out, a, b, op):
+        run("v", lambda: g.vector.tensor_tensor(out[0], a[0], b[0], op), [out], [a, b])
+
+    def fill(out, c):
+        run("v", lambda: g.vector.memset(out[0], c), [out], [])
+
+    def turn(out, in_):
+        run("v", lambda: g.vector.transpose(out[0], in_[0]), [out], [in_])
+
+    def quant(q, s, in_):
+        run("v", lambda: g.vector.quantize_mx(q[0], s[0], in_[0]), [q, s], [in_])
+
+    def mm(out, l, ls, r, rs):
+        run("t", lambda: g.tensor.matmul_mx(out[0], l[0], ls[0], r[0], rs[0], True, True), [out], [l, ls, r, rs])
+
+    def iota(out, pattern, base, cm, f=False):
+        if f:
+            run("p", lambda: g.iota(out[0], pattern, base, cm, allow_small_or_imprecise_dtypes=True), [out], [])
+        else:
+            run("p", lambda: g.iota(out[0], pattern, base, cm), [out], [])
+
+    def scan(out, in_):
+        d = A("d")
+        run("v", lambda: g.vector.tensor_tensor_scan(out[0], in_[0], d[0], -BIG, ALU.max, ALU.add), [out], [in_, d])
+
+    def wrapped(name, p=None):
+        return A(name, 15, 448, 16, p)
+
+    def bank(c, t, n):
+        return A(("pa", "pb")[c % 2], 512 * t, 512 * t + n)
+
+    def score(i, n):
+        return A(("pb", "pa")[i // 4], 512 * (i % 4), 512 * (i % 4) + n)
+
+    spare = []
+
+    def gap(n=1):
+        while n and spare:
+            spare.pop(0)()
+            n -= 1
+
+    dma("y", A("gli"), ext(T.gl[:, :]), "dgl")
+    dma("s", A("hti"), ext(T.ht[:, :]), "dht")
+    for k, (a, b) in enumerate(CHL):
+        dma("s" if k == 0 else "y", A("x0", 4 * a, 4 * b), ext(T.x[:, 4 * a:4 * b]), "dx%d" % k)
+    dma("y", A("ut"), ext(T.u[:, :]), "du")
+    waits("y", A("x0")[1] + A("ut")[1], [])
+    dma("y", A("qws"), ext(T.ws[:, :]), "dw")
+    dma("y", A("qw", cast=dt.uint8), ext(T.wc[:, :]), "dw")
+    dma("y", A("vt"), ext(T.v[:, :]), "dv")
+
+    for k in range(4):
+        spare.append(lambda k=k: fill(A("ec", 512 * k, 512 * k + 512), 0.0))
+    fill(A("eye"), 1.0)
+    iota(A("m16"), [[1, 16]], 0, 0, True)
+    iota(A("pi"), [[0, 1]], 0, 1)
+    iota(A("uli"), [[16, 2], [32, 4], [0, 2]], 0, 0)
+    run("p", lambda: g.affine_select(T.eye[:, :], T.eye[:, :], [[-1, 128]], ALU.is_equal, 0.0, 0, 1), [A("eye")], [A("eye")])
+    iota(A("idl"), [[16, 28]], 0, 1)
+    iota(A("wb", 0, 448), [[1, 448]], 0, 0, True)
+    fill(A("wt"), 0.0)
+    fill(A("l2"), 0)
+    gap(2)
+    ts(A("lo"), A("pi"), 15, ALU.bitwise_and)
+    ts(A("hi"), A("pi"), 4, ALU.logical_shift_right, 1, ALU.bitwise_and)
+    ts(A("dc"), A("m16"), 15.0, ALU.is_equal, -2.0, ALU.mult)
+    copy(A("ul"), A("uli"))
+    copy(A("lof"), A("lo"))
+    ts(A("off"), A("hi"), 448.0, ALU.mult, BIG, ALU.add)
+    gap()
+    ts(A("da"), A("m16"), A("lof"), ALU.is_ge)
+    ts(A("db"), A("m16"), A("lof"), ALU.is_equal)
+    gap()
+    tt(A("dd"), A("da"), A("db"), ALU.add)
+    for t in range(4):
+        copy(A("ec", 513 * t, 512 * t + 512, 4), A("eye"), "s")
+    copy(A("wt", 0, 56), A("gli"))
+    tt(A("de"), A("dd"), A("dc"), ALU.add)
+    turn(A("tg", 0, 64), A("wt", 0, 64))
+    turn(A("tg", 64, 128), A("wt", 0, 64))
+    ts(A("d", 0, 16), A("de"), -1.0, ALU.add, BIG, ALU.mult)
+    w = [16]
+
+    def widen():
+        if w[0] < C:
+            n = min(w[0], C - w[0])
+            copy(A("d", w[0], w[0] + n), A("d", 0, n))
+            w[0] += n
+
+    for k in (0, 32):
+        copy(A("tg", k + 16, k + 32), A("tg", k, k + 16))
+        copy(A("tg", 64 + k, 64 + k + 16), A("tg", 64 + k + 16, 64 + k + 32))
+    widen()
+    turn(A("tg2"), A("tg"))
+    widen()
+    copy(A("gs", 0, 56), A("tg2", 0, 56))
+    copy(A("gs", 56, 112), A("tg2", 64, 120))
+    send(1, A("gr1"), A("gs"), "g1")
+    send_both()
+    for s in STEPS:
+        arrives(s, A("gr%d" % s), "g%d" % s, 1 if s == 1 else 2)
+    copy(A("wt", 64, 92), A("hti"))
+    for t in range(4):
+        ts(A("hl", 28 * t, 28 * t + 28), A("hti"), 4.0, ALU.mult, float(t), ALU.add)
+    turn(A("th", 0, 32), A("wt", 64, 96))
+    turn(A("th", 32, 64), A("wt", 64, 96))
+    widen()
+    widen()
+    copy(A("th", 16, 32), A("th", 0, 16))
+    copy(A("th", 32, 48), A("th", 48, 64))
+    widen()
+    turn(A("th2"), A("th"))
+    quant(A("qe"), A("qes"), A("ec"))
+    copy(A("hx", 0, 28), A("th2", 0, 28))
+    copy(A("hx", 28, 56), A("th2", 32, 60))
+    quant(A("qu"), A("qus"), A("ut"))
+    ul = A("ul")
+    copy(A("qps"), A("qus", by=ul), "s")
+    copy(A("qp", cast=dt.uint32), A("qu", cast=dt.uint32, by=ul))
+
+    def nature(s, wave):
+        nat = ("na%d", "nb%d")[wave] % (s % 2)
+        lst = 56 * wave
+        if s == 1 and wave == 0:
+            copy(A(nat, 0, 448), A("wb", 0, 448, by=A("gr1", 0, 28)))
+            copy(A(nat, 448, 896), A("wb", 0, 448, by=A("gr1", 28, 56)), "s")
+        else:
+            copy(A(nat), A("wb", 0, 448, by=A("gr%d" % s, lst, lst + 56)), "s")
+        if wave:
+            scaled(A(nat, 0, 896, 2), A(nat, 0, 896, 2), 1024.0)
+
+    def join(s, wave, a, b):
+        nat = ("na%d", "nb%d")[wave] % (s % 2)
+        tt(A(("ea%d", "eb%d")[wave] % s, a, b), A(nat, 2 * a + 1, 2 * b, 2), A(nat, 2 * a, 2 * b, 2), (ALU.subtract, ALU.add)[wave])
+
+    def even(s):
+        scan(A("gw"), A("na%d" % (s % 2), 0, 896, 2))
+
+    def halves(out, a, b, name):
+        copy(A(out, a, a + 224), A("wb", 0, b, by=A(name, 0, 14)))
+        copy(A(out, a + 224, a + 448), A("wb", 0, b, by=A(name, 14, 28)), "s")
+
+    def settle(s, c):
+        a, b = CHZ[c]
+        q, sc = A("qx%d" % s, a, b), A("qxs%d" % s, a, b)
+        quant(q, sc, A("x%d" % s, 4 * a, 4 * b))
+        if s < 3:
+            mm(score(c, b - a), A("qp", 0, 128), A("qps", 0, 128), q, sc)
+        else:
+            mm(score(c, b - a), A("qv"), A("qvs"), q, sc)
+            if c:
+                a, b = CHL[c - 1]
+                dma("y", ext(T.oc[:, 4 * a:4 * b]), A("qx3", a, b, cast=dt.uint8), "oo")
+
+    for c in range(3):
+        settle(0, c)
+    for s in STEPS:
+        k = "%d" % s
+        xo, xn = "x%d" % (s - 1), "x" + k
+        qx, qxs = "qx%d" % (s - 1), "qxs%d" % (s - 1)
+        first = s == 1
+        for a in range(0, 1792, 448):
+            spare.append(lambda a=a: ts(A("x64", a, a + 448), A(xo, a, a + 448), 64.0, ALU.mult))
+        if s < 3:
+            for a in range(0, C, PIECE):
+                spare.append(lambda a=a: join(s + 1, 0, a, a + PIECE))
+
+        def host_gather(c, which):
+            a, b = CHH[c]
+            for t in which:
+                copy(A("h" + k, 4 * a + t, 4 * b, 4), A(xo, by=A("hl", 28 * t + a // 16, 28 * t + b // 16)), "s")
+
+        def host_send(c):
+            a, b = CHH[c]
+            quant(A("qh" + k, a, b), A("qhs" + k, a, b), A("h" + k, 4 * a, 4 * b))
+            sem = "c" + k + "ab"[c]
+            send(s, A("hc" + k, a, b, cast=dt.uint8), A("qh" + k, a, b, cast=dt.uint8), sem)
+            send(s, A("hcs" + k, a, b), A("qhs" + k, a, b), sem)
+            arrives(s, A("hc" + k, a, b), sem)
+            arrives(s, A("hcs" + k, a, b), sem)
+
+        def bits(n, c):
+            a, b = CHZ[c]
+            if n == 0:
+                ts(A("b2", a, b), score(c, b - a), 0.0, ALU.is_gt)
+            else:
+                ts(A("b1", a, b), score(3 + c, b - a), 0.0, ALU.is_gt, 2.0 ** -10, ALU.max)
+
+        for c, (a, b) in enumerate(CHZ):
+            mm(score(3 + c, b - a), A("qp", 128, 256), A("qps", 128, 256), A(qx, a, b), A(qxs, a, b))
+        if first:
+            host_gather(0, (0,))
+            nature(1, 0)
+            host_gather(0, (1, 2, 3))
+            nature(1, 1)
+        else:
+            host_gather(0, range(4))
+        host_gather(1, range(4))
+        for c in range(3):
+            bits(0, c)
+        if first:
+            join(1, 0, 0, 224)
+            join(1, 0, 224, 448)
+            bits(1, 0)
+        tt(A("t2"), A("b2", by=A("hx", 0, 28)), A("ea" + k), ALU.mult)
+        host_send(0)
+        scan(A("s2"), A("t2"))
+        if first:
+            bits(1, 1)
+            bits(1, 2)
+            even(1)
+        else:
+            bits(1, 0)
+        tt(A("lf"), wrapped("s2"), wrapped("gw"), ALU.add)
+        if first:
+            join(1, 1, 0, 224)
+        else:
+            bits(1, 1)
+        ts(A("l1"), A("lf"), 2 * BIG, ALU.add)
+        if first:
+            join(1, 1, 224, 448)
+            host_send(1)
+        else:
+            bits(1, 2)
+        tt(A("t1"), A("b1", by=A("hx", 28, 56)), A("eb" + k), ALU.mult)
+        copy(A("wb", 448, 896), A("wb", 0, 448, by=A("l1")), "s")
+        if first:
+            nature(2, 0)
+            gap()
+        else:
+            host_send(1)
+        ts(A("n1"), A("t1"), 1023, ALU.bitwise_and)
+        copy(A("l3", p=(0, 32)), A("l1", p=(0, 32)))
+        gap()
+        copy(A("wb", 896, 1344), A("n1", by=A("l1")))
+        copy(A("l3", p=(0, 16)), A("idl", p=(0, 16)))
+        gap()
+        scan(A("s3"), A("wb", 896, 1344))
+        gap()
+        ts(A("l2", p=(32, 64)), wrapped("s3", (0, 32)), BIG + 896.0, ALU.add)
+        ts(A("l2", p=(96, 128)), wrapped("s3", (64, 96)), A("off", p=(64, 96)), ALU.add)
+        ts(A("l3", p=(32, 64)), wrapped("s3", (0, 32)), A("off", p=(0, 32)), ALU.add)
+        if s < 3:
+            gap()
+        halves("wb", 1344, 1344, "l2")
+        gap()
+        scan(A("s4"), A("wb", 1344, 1792))
+        gap()
+        ts(A("l3", p=(64, 96)), wrapped("s4", (32, 64)), A("off", p=(32, 64)), ALU.add)
+        ts(A("l3", p=(96, 128)), wrapped("s4", (32, 64)), BIG + 1344.0, ALU.add)
+        gap()
+        halves("o5", 0, 1792, "l3")
+        if first:
+            nature(2, 1)
+            nature(3, 0)
+        elif s == 2:
+            nature(3, 1)
+        gap()
+        scan(A("s5"), A("o5"))
+        gap()
+        ts(A("vl" + k), wrapped("s5"), BIG, ALU.add)
+        send(s, A("vr" + k), A("vl" + k), "k" + k)
+        arrives(s, A("vr" + k), "k" + k)
+        gap(len(spare))
+        if s < 3:
+            even(s + 1)
+        for c, (a, b) in enumerate(CHH):
+            for t in range(4):
+                mm(bank(c, t, b - a), A("qe", 128 * t, 128 * t + 128), A("qes", 128 * t, 128 * t + 128), A("hc" + k, a, b), A("hcs" + k, a, b))
+            for t in range(4):
+                tt(A("m" + k, 448 * t + a, 448 * t + b), A(xo, 4 * a + t, 4 * b, 4), bank(c, t, b - a), ALU.max)
+            if s == 3 and c == 0:
+                copy(A("o8"), A("n1", by=A("vl" + k)))
+        if s == 3:
+            scan(A("s8"), A("o8"))
+            quant(A("qv"), A("qvs"), A("vt"))
+            ts(A("l8"), wrapped("s8"), BIG, ALU.add)
+            send(s, A("r8"), A("l8"), "k8")
+            arrives(s, A("r8"), "k8")
+        else:
+            join(s + 1, 1, 0, 224)
+
+        def mosaic(c, t, q):
+            a, b = CHZ[c]
+            copy(A("z" + k, 4 * a + t, 4 * b, 4), A("m" + k, 448 * t, 448 * t + 448, by=A("vr" + k, a // 16, b // 16)), q)
+
+        def layer(c):
+            a, b = CHZ[c]
+            quant(A("qz" + k, a, b), A("qzs" + k, a, b), A("z" + k, 4 * a, 4 * b))
+            for t in range(4):
+                mm(bank(c, t, b - a), A("qw", 128 * t, 128 * t + 128), A("qws", 128 * t, 128 * t + 128),
+                   A("qz" + k, a, b), A("qzs" + k, a, b))
+
+        def finish(c):
+            a, b = CHZ[c]
+            for t in range(4):
+                tt(A("tmp", 448 * t + a, 448 * t + b), bank(c, t, b - a), A("x64", 4 * a + t, 4 * b, 4), ALU.add)
+                scaled(A(xn, 4 * a + t, 4 * b, 4), A("tmp", 448 * t + a, 448 * t + b), 2.0 ** -6)
+
+        for c in range(3):
+            mosaic(c, 2, "s")
+            mosaic(c, 3, "s")
+        mosaic(2, 1, "s")
+        if s == 3:
+            copy(A("p7"), A("wb", 0, 448, by=A("vr3")), "s")
+            dma("y", ext(T.pl[0:7, :]), (T.p7[16:128:16, :], A("p7")[1]), "op_")
+        mosaic(0, 0, "v")
+        mosaic(0, 1, "v")
+        mosaic(1, 0, "v")
+        layer(0)
+        mosaic(1, 1, "v")
+        mosaic(2, 0, "v")
+        layer(1)
+        finish(0)
+        layer(2)
+        finish(1)
+        finish(2)
+        for c in range(3):
+            settle(s, c)
+        if s < 3:
+            join(s + 1, 1, 224, 448)
+
+    for i in range(4):
+        dma("y", ext(T.osc[4 * i:4 * i + 4, :]), A("qxs3", p=(32 * i, 32 * i + 4)), "os_")
+    for c, (a, b) in enumerate(CHZ):
+        copy(A("yb", a, b), score(c, b - a), "ssv"[c])
+    dma("y", ext(T.y[:, :]), A("yb"), "oy")
+    copy(A("p8"), A("wb", 0, 448, by=A("r8")), "s")
+    dma("s", ext(T.pl[7:8, :]), A("p8", p=(112, 113)), "op_")
+    for sem in sorted(total):
+        if seen["p"].get(sem, 0) < total[sem]:
+            g.wait_ge(T.sem[sem], total[sem])

@@ -3,14 +3,15 @@ from concourse.mybir import dt, AluOpType, ActivationFunctionType
 
 C = 448
 STEPS = (1, 2, 3)
-CHH = ((0, 224), (224, 448))
-CHZ = ((0, 160), (160, 320), (320, 448))
+CH = ((0, 160), (160, 320), (320, 448))
 CHL = ((0, 320), (320, 448))
-PIECE = 112
-BIG = 524288.0
+CHH = ((0, 224), (224, 448))
+BIG = 512.0
+MID = 224.0
+TOP = 240.0
 ALU = AluOpType
-COPY = ActivationFunctionType.Copy
-F8, U8, BF, F32, I32, U16 = "float8_e4m3fn_x4", "uint8", "bfloat16", "float32", "int32", "uint16"
+ACT = ActivationFunctionType
+F8, U8, BF, F32, I32, U16, F16 = "float8_e4m3fn_x4", "uint8", "bfloat16", "float32", "int32", "uint16", "float16"
 
 SCRATCH = {"pa": ("psum", [128, 2048], F32), "pb": ("psum", [128, 2048], F32)}
 
@@ -20,26 +21,25 @@ def _sbuf(kind, **widths):
         SCRATCH[name] = ("sbuf", [128, widths[name]], kind)
 
 
-_sbuf(I32, gli=56, hti=28, uli=16, pi=1, lo=1, hi=1, idl=28, t1=448, n1=448)
-_sbuf(U16, gs=112, hx=56, hl=112, ul=16, l1=28, l2=28, l3=28, l8=28, r8=28)
-_sbuf(BF, ut=512, vt=512, ec=2048, eye=128, x64=1792)
+_sbuf(I32, gli=112, hti=56, uli=16, ulm=16, pi=1, ci=2)
+_sbuf(U16, glu=112, hu=56, hl=112, ul=16, lw=28, l1=28, l2=28, l3=28, vl=28, l8=28)
+_sbuf(BF, ut=512, vt=512, ec=2048, eye=128, pat=32, ini=2, idb=448, db=448, dw=448, gt=896, gn=896, bt=448, bl=448,
+      at=448, al=448, t0=448, pw=896, p2=448)
+_sbuf(F16, st=448, sl=448, s1=448, s2=448, s3=448)
 _sbuf(F8, qu=128, qp=256, qv=128, qe=512, qw=512)
 _sbuf(U8, qus=128, qps=256, qvs=128, qes=512, qws=512)
-_sbuf(F32, wt=96, tg=128, tg2=128, th=64, th2=64, lof=1, off=1, m16=16, da=16, db=16, dc=16, dd=16, de=16, d=448, gw=448,
-      wb=1792, b1=448, b2=448, t2=448, s2=448, s3=448, s4=448, o5=448, s5=448, lf=28, na0=896, nb0=896, na1=896, nb1=896,
-      tmp=1792, o8=448, s8=448, p7=448, p8=448, yb=448)
+_sbuf(F32, cf=2, col=2, mm=16, e=16, ea=16, eb=16, i8=56, i32=28, kk=28, kc=28, dl=28, cl=28, la=28, lb=28, p8=448, yb=448)
 for _k in range(4):
-    SCRATCH["x%d" % _k] = ("sbuf", [128, 1792], BF)
-    SCRATCH["qx%d" % _k] = ("sbuf", [128, 448], F8)
-    SCRATCH["qxs%d" % _k] = ("sbuf", [128, 448], U8)
+    for _n, _w, _d in (("x", 1792, BF), ("k", 1792, BF), ("qx", 448, F8), ("qxs", 448, U8)):
+        SCRATCH["%s%d" % (_n, _k)] = ("sbuf", [128, _w], _d)
 for _k in STEPS:
     for _n, _w, _d in (("h", 1792, BF), ("m", 1792, BF), ("z", 1792, BF), ("qh", 448, F8), ("hc", 448, F8), ("qz", 448, F8),
-                       ("qhs", 448, U8), ("hcs", 448, U8), ("qzs", 448, U8), ("vl", 28, U16), ("vr", 28, U16), ("gr", 112, U16),
-                       ("ea", 448, F32), ("eb", 448, F32)):
+                       ("qhs", 448, U8), ("hcs", 448, U8), ("qzs", 448, U8), ("it", 28, U16), ("ir", 28, U16),
+                       ("ib", 28, BF), ("br", 28, BF)):
         SCRATCH["%s%d" % (_n, _k)] = ("sbuf", [128, _w], _d)
-SEMAPHORES = ["v", "s", "t", "p", "rl", "k8", "dgl", "dht", "dx0", "dx1", "du", "dw", "dv", "oo", "os_", "oy", "op_"]
+SEMAPHORES = ["v", "s", "t", "p", "rl", "dgl", "dht", "dx0", "dx1", "dh2", "du", "dw", "dv", "oo", "os_", "oy", "op_"]
 for _k in STEPS:
-    SEMAPHORES += ["g%d" % _k, "k%d" % _k, "c%da" % _k, "c%db" % _k]
+    SEMAPHORES += ["k%d" % _k, "c%d0" % _k, "c%d1" % _k]
 
 
 def rank_program(g, core, T, topo):
@@ -111,49 +111,37 @@ def rank_program(g, core, T, topo):
     def ext(view):
         return view, []
 
-    def core_of(step):
-        return T.cores[rank ^ step]
-
-    def send(step, out, in_, sem):
-        dst = core_of(step)
-        waits("p", in_[1], [])
+    def send(step, moves, sem):
+        dst = T.cores[rank ^ step]
         rid, pid, _ = topo.addr(dst)
-        g.remote_dma(out[0], in_[0], T.sem[sem], T.sem.rl, pid, rid, topo.mask(core, dst))
-        total["rl"] = total.get("rl", 0) + len(topo.engines(core, dst))
-
-    def send_both():
+        eng = topo.engines(core, dst)
+        n = len(eng) // len(moves)
         mv = []
-        waits("p", A("gs")[1], [])
-        for j, st in enumerate((2, 3)):
-            dst = core_of(st)
-            rid, pid, _ = topo.addr(dst)
-            eng = topo.engines(core, dst)
-            mine = eng[len(eng) // 2 * j:len(eng) // 2 * (j + 1)]
-            mv.append(RemoteDMATransfer(dst_ids=[DstId(rid=rid, pnc=pid)], dma_engine_mask=sum(1 << e for e in mine),
-                                        remote_sem=T.sem["g%d" % st], src=T.gs[:, :], dst=T["gr%d" % st][:, :]))
-            total["rl"] = total.get("rl", 0) + len(mine)
+        for j, (out, in_) in enumerate(moves):
+            waits("p", in_[1], [])
+            mv.append(RemoteDMATransfer(dst_ids=[DstId(rid=rid, pnc=pid)], dma_engine_mask=sum(1 << e for e in eng[n * j:n * j + n]),
+                                        remote_sem=T.sem[sem], src=in_[0], dst=out[0]))
+            note([], out[1], sem, None)
         g.remote_dma_fused(mv, local_sem=T.sem.rl)
+        total["rl"] = total.get("rl", 0) + len(eng)
+        total[sem] = total.get(sem, 0) + len(topo.engines(dst, core))
 
-    def arrives(step, out, sem, part=1):
-        total[sem] = total.get(sem, 0) + len(topo.engines(core_of(step), core)) // part
-        note([], out[1], sem, None)
+    def act(out, in_, func=ACT.Copy, **kw):
+        run("s", lambda: g.scalar.activation(out[0], in_[0], func, **kw), [out], [in_])
 
     def copy(out, in_, q="v"):
         if q == "v":
             run("v", lambda: g.vector.tensor_copy(out[0], in_[0]), [out], [in_])
         else:
-            run("s", lambda: g.scalar.activation(out[0], in_[0], COPY), [out], [in_])
-
-    def scaled(out, in_, c):
-        run("s", lambda: g.scalar.activation(out[0], in_[0], COPY, scale=c), [out], [in_])
+            act(out, in_)
 
     def ts(out, in_, a, op0, b=None, op1=None):
-        col = [a] if isinstance(a, tuple) else []
-        a0 = a[0] if col else a
+        col = [c for c in (a, b) if isinstance(c, tuple)]
+        a0, b0 = [c[0] if isinstance(c, tuple) else c for c in (a, b)]
         if op1 is None:
             run("v", lambda: g.vector.tensor_scalar(out[0], in_[0], a0, None, op0), [out], [in_] + col)
         else:
-            run("v", lambda: g.vector.tensor_scalar(out[0], in_[0], a0, b, op0, op1), [out], [in_] + col)
+            run("v", lambda: g.vector.tensor_scalar(out[0], in_[0], a0, b0, op0, op1), [out], [in_] + col)
 
     def tt(out, a, b, op):
         run("v", lambda: g.vector.tensor_tensor(out[0], a[0], b[0], op), [out], [a, b])
@@ -161,33 +149,45 @@ def rank_program(g, core, T, topo):
     def fill(out, c):
         run("v", lambda: g.vector.memset(out[0], c), [out], [])
 
-    def turn(out, in_):
-        run("v", lambda: g.vector.transpose(out[0], in_[0]), [out], [in_])
-
     def quant(q, s, in_):
         run("v", lambda: g.vector.quantize_mx(q[0], s[0], in_[0]), [q, s], [in_])
 
     def mm(out, l, ls, r, rs):
         run("t", lambda: g.tensor.matmul_mx(out[0], l[0], ls[0], r[0], rs[0], True, True), [out], [l, ls, r, rs])
 
-    def iota(out, pattern, base, cm, f=False):
+    def iota(out, pattern, base, cm, f=True):
         if f:
             run("p", lambda: g.iota(out[0], pattern, base, cm, allow_small_or_imprecise_dtypes=True), [out], [])
         else:
             run("p", lambda: g.iota(out[0], pattern, base, cm), [out], [])
 
-    def scan(out, in_):
-        d = A("d")
-        run("v", lambda: g.vector.tensor_tensor_scan(out[0], in_[0], d[0], -BIG, ALU.max, ALU.add), [out], [in_, d])
+    def scan(out, in_, d, first=-BIG):
+        col = [first] if isinstance(first, tuple) else []
+        f0 = first[0] if col else first
+        run("v", lambda: g.vector.tensor_tensor_scan(out[0], in_[0], d[0], f0, ALU.max, ALU.add), [out], [in_, d] + col)
 
     def wrapped(name, p=None):
         return A(name, 15, 448, 16, p)
+
+    def column(i, p=None):
+        return A("col", i, i + 1, p=p)
 
     def bank(c, t, n):
         return A(("pa", "pb")[c % 2], 512 * t, 512 * t + n)
 
     def score(i, n):
-        return A(("pb", "pa")[i // 4], 512 * (i % 4), 512 * (i % 4) + n)
+        return A("pb", 512 * i, 512 * i + n)
+
+    def shared(out, a, win, lst, cut, relu=False, base=0, n=28):
+        for q, i, j in (("v", 0, cut), ("s", cut, n)):
+            if i < j:
+                o, w = A(out, a + 16 * i, a + 16 * j), A(win[0], win[1], win[2], by=A(lst, base + i, base + j))
+                if not relu:
+                    copy(o, w, q)
+                elif q == "v":
+                    ts(o, w, 0.0, ALU.max)
+                else:
+                    act(o, w, ACT.Relu)
 
     spare = []
 
@@ -196,294 +196,247 @@ def rank_program(g, core, T, topo):
             spare.pop(0)()
             n -= 1
 
-    dma("y", A("gli"), ext(T.gl[:, :]), "dgl")
-    dma("s", A("hti"), ext(T.ht[:, :]), "dht")
-    for k, (a, b) in enumerate(CHL):
-        dma("s" if k == 0 else "y", A("x0", 4 * a, 4 * b), ext(T.x[:, 4 * a:4 * b]), "dx%d" % k)
+    def turned(q, name, a, w, src, sem):
+        dma(q, A(name, a, a + w, p=(16, 128)), ext(src[0:112, :]), sem)
+        dma(q, A(name, a, a + w, p=(0, 16)), ext(src[112:128, :]), sem)
+
     dma("y", A("ut"), ext(T.u[:, :]), "du")
-    waits("y", A("x0")[1] + A("ut")[1], [])
+    dma("s", A("hti", 0, 28), ext(T.ht[:, :]), "dht")
+    for c, (a, b) in enumerate(CHL):
+        dma("y", A("x0", 4 * a, 4 * b), ext(T.x[:, 4 * a:4 * b]), "dx%d" % c)
+    turned("s", "hti", 28, 28, T.ht, "dh2")
+    turned("y", "gli", 0, 56, T.gl, "dgl")
+    dma("y", A("gli", 56, 112), ext(T.gl[:, :]), "dgl")
+    waits("y", A("x0")[1], [])
     dma("y", A("qws"), ext(T.ws[:, :]), "dw")
     dma("y", A("qw", cast=dt.uint8), ext(T.wc[:, :]), "dw")
-    dma("y", A("vt"), ext(T.v[:, :]), "dv")
 
+    g0 = (0, 16)
+    iota(A("pi"), [[0, 1]], 0, 1, False)
+    iota(A("mm"), [[1, 16]], 0, 0)
+    iota(A("uli"), [[-16, 2], [16, 8]], 112, 0, False)
+    iota(A("i8"), [[8, 56]], 0, 0)
+    fill(A("eye"), 1.0)
+    iota(A("i32"), [[32, 28]], -1024, 0)
+    run("p", lambda: g.affine_select(T.eye[:, :], T.eye[:, :], [[-1, 128]], ALU.is_equal, 0.0, 0, 1), [A("eye")], [A("eye")])
+    iota(A("kk"), [[-32, 28]], 1536, 0)
+    iota(A("idb"), [[1, 448]], -224, 0)
     for k in range(4):
         spare.append(lambda k=k: fill(A("ec", 512 * k, 512 * k + 512), 0.0))
-    fill(A("eye"), 1.0)
-    iota(A("m16"), [[1, 16]], 0, 0, True)
-    iota(A("pi"), [[0, 1]], 0, 1)
-    iota(A("uli"), [[16, 2], [32, 4], [0, 2]], 0, 0)
-    run("p", lambda: g.affine_select(T.eye[:, :], T.eye[:, :], [[-1, 128]], ALU.is_equal, 0.0, 0, 1), [A("eye")], [A("eye")])
-    iota(A("idl"), [[16, 28]], 0, 1)
-    iota(A("wb", 0, 448), [[1, 448]], 0, 0, True)
-    fill(A("wt"), 0.0)
-    fill(A("l2"), 0)
-    gap(2)
-    ts(A("lo"), A("pi"), 15, ALU.bitwise_and)
-    ts(A("hi"), A("pi"), 4, ALU.logical_shift_right, 1, ALU.bitwise_and)
-    ts(A("dc"), A("m16"), 15.0, ALU.is_equal, -2.0, ALU.mult)
-    copy(A("ul"), A("uli"))
-    copy(A("lof"), A("lo"))
-    ts(A("off"), A("hi"), 448.0, ALU.mult, BIG, ALU.add)
     gap()
-    ts(A("da"), A("m16"), A("lof"), ALU.is_ge)
-    ts(A("db"), A("m16"), A("lof"), ALU.is_equal)
+    ts(A("ci", 0, 1), A("pi"), 15, ALU.bitwise_and)
+    ts(A("ci", 1, 2), A("pi"), 15, ALU.bitwise_and, 1, ALU.logical_shift_right)
+    fill(A("ini"), -BIG)
+    fill(column(1), BIG + MID)
+    copy(A("cf"), A("ci"))
+    fill(column(1, g0), -TOP)
+    ts(A("ulm"), A("uli"), 127, ALU.bitwise_and)
+    i1 = A("cf", 0, 1)
+    ts(A("e"), A("mm"), i1, ALU.subtract)
+    ts(A("lw"), A("i8", 0, 28), 0.0, ALU.mult, i1, ALU.add)
+    copy(A("ul"), A("ulm"))
+    ts(A("ea"), A("e"), 0.0, ALU.is_equal, BIG, ALU.mult)
+    ts(A("eb"), A("e"), 0.0, ALU.is_lt, -BIG, ALU.mult)
     gap()
-    tt(A("dd"), A("da"), A("db"), ALU.add)
+    tt(A("e"), A("ea"), A("eb"), ALU.add)
+    ts(column(0), i1, 2.0, ALU.mult, 3 * BIG, ALU.add)
+    ts(A("ini", 0, 1, p=g0), A("cf", 0, 1, p=g0), TOP - 16, ALU.add)
+    ts(A("e", 15, 16), A("e", 15, 16), -2 * BIG, ALU.add)
+    gap()
+    copy(A("pat", 0, 16), A("e"))
+    copy(A("pat", 16, 32), A("e"))
+    gap()
+    copy(A("db"), A("pat", 0, 16, by=A("lw")), "s")
+    fill(A("pat", 16, 32, p=g0), 0.0)
     for t in range(4):
-        copy(A("ec", 513 * t, 512 * t + 512, 4), A("eye"), "s")
-    copy(A("wt", 0, 56), A("gli"))
-    tt(A("de"), A("dd"), A("dc"), ALU.add)
-    turn(A("tg", 0, 64), A("wt", 0, 64))
-    turn(A("tg", 64, 128), A("wt", 0, 64))
-    ts(A("d", 0, 16), A("de"), -1.0, ALU.add, BIG, ALU.mult)
-    w = [16]
-
-    def widen():
-        if w[0] < C:
-            n = min(w[0], C - w[0])
-            copy(A("d", w[0], w[0] + n), A("d", 0, n))
-            w[0] += n
-
-    for k in (0, 32):
-        copy(A("tg", k + 16, k + 32), A("tg", k, k + 16))
-        copy(A("tg", 64 + k, 64 + k + 16), A("tg", 64 + k + 16, 64 + k + 32))
-    widen()
-    turn(A("tg2"), A("tg"))
-    widen()
-    copy(A("gs", 0, 56), A("tg2", 0, 56))
-    copy(A("gs", 56, 112), A("tg2", 64, 120))
-    send(1, A("gr1"), A("gs"), "g1")
-    send_both()
-    for s in STEPS:
-        arrives(s, A("gr%d" % s), "g%d" % s, 1 if s == 1 else 2)
-    copy(A("wt", 64, 92), A("hti"))
-    for t in range(4):
-        ts(A("hl", 28 * t, 28 * t + 28), A("hti"), 4.0, ALU.mult, float(t), ALU.add)
-    turn(A("th", 0, 32), A("wt", 64, 96))
-    turn(A("th", 32, 64), A("wt", 64, 96))
-    widen()
-    widen()
-    copy(A("th", 16, 32), A("th", 0, 16))
-    copy(A("th", 32, 48), A("th", 48, 64))
-    widen()
-    turn(A("th2"), A("th"))
-    quant(A("qe"), A("qes"), A("ec"))
-    copy(A("hx", 0, 28), A("th2", 0, 28))
-    copy(A("hx", 28, 56), A("th2", 32, 60))
+        ts(A("hl", 28 * t, 28 * t + 28), A("hti", 0, 28), 4.0, ALU.mult, float(t), ALU.add)
+    fill(A("pat", 16, 17, p=g0), 16.0)
     quant(A("qu"), A("qus"), A("ut"))
+    for r in range(4):
+        q = (r - 1) % 4
+        copy(A("hu", 28, 56, p=(32 * r, 32 * r + 32)), A("hti", 0, 28, p=(32 * q, 32 * q + 32)))
     ul = A("ul")
     copy(A("qps"), A("qus", by=ul), "s")
     copy(A("qp", cast=dt.uint32), A("qu", cast=dt.uint32, by=ul))
-
-    def nature(s, wave):
-        nat = ("na%d", "nb%d")[wave] % (s % 2)
-        lst = 56 * wave
-        if s == 1 and wave == 0:
-            copy(A(nat, 0, 448), A("wb", 0, 448, by=A("gr1", 0, 28)))
-            copy(A(nat, 448, 896), A("wb", 0, 448, by=A("gr1", 28, 56)), "s")
-        else:
-            copy(A(nat), A("wb", 0, 448, by=A("gr%d" % s, lst, lst + 56)), "s")
-        if wave:
-            scaled(A(nat, 0, 896, 2), A(nat, 0, 896, 2), 1024.0)
-
-    def join(s, wave, a, b):
-        nat = ("na%d", "nb%d")[wave] % (s % 2)
-        tt(A(("ea%d", "eb%d")[wave] % s, a, b), A(nat, 2 * a + 1, 2 * b, 2), A(nat, 2 * a, 2 * b, 2), (ALU.subtract, ALU.add)[wave])
-
-    def even(s):
-        scan(A("gw"), A("na%d" % (s % 2), 0, 896, 2))
-
-    def halves(out, a, b, name):
-        copy(A(out, a, a + 224), A("wb", 0, b, by=A(name, 0, 14)))
-        copy(A(out, a + 224, a + 448), A("wb", 0, b, by=A(name, 14, 28)), "s")
+    ts(A("db", 15, 448, 16), A("i32"), A("pat", 15, 16), ALU.add)
+    for t in range(4):
+        copy(A("ec", 513 * t, 512 * t + 512, 4), A("eye"), "s")
+    ts(A("glu", 56, 112, p=(0, 32)), A("i8", p=(0, 32)), A("cf", 1, 2, p=(0, 32)), ALU.add)
+    ts(A("l2"), A("i8", 0, 28), 2.0, ALU.mult, i1, ALU.add)
+    ts(A("l3"), A("i8", 0, 28), 2.0, ALU.mult, i1, ALU.add)
+    ts(A("kc"), A("kk"), MID, ALU.add)
+    ts(A("l8"), A("l2"), 448.0, ALU.add)
+    copy(A("hu", 0, 28), A("hti", 28, 56))
 
     def settle(s, c):
-        a, b = CHZ[c]
-        q, sc = A("qx%d" % s, a, b), A("qxs%d" % s, a, b)
-        quant(q, sc, A("x%d" % s, 4 * a, 4 * b))
-        if s < 3:
-            mm(score(c, b - a), A("qp", 0, 128), A("qps", 0, 128), q, sc)
-        else:
-            mm(score(c, b - a), A("qv"), A("qvs"), q, sc)
-            if c:
-                a, b = CHL[c - 1]
+        a, b = CH[c]
+        quant(A("qx%d" % s, a, b), A("qxs%d" % s, a, b), A("x%d" % s, 4 * a, 4 * b))
+        if c:
+            a, b = CHL[c - 1]
+            q, sc = A("qx%d" % s, a, b), A("qxs%d" % s, a, b)
+            if s < 3:
+                for w in range(2):
+                    mm(score(2 * c - 2 + w, b - a), A("qp", 128 * w, 128 * w + 128), A("qps", 128 * w, 128 * w + 128), q, sc)
+            else:
+                mm(score(c - 1, b - a), A("qv"), A("qvs"), q, sc)
                 dma("y", ext(T.oc[:, 4 * a:4 * b]), A("qx3", a, b, cast=dt.uint8), "oo")
+
+    def signs(c, w, q):
+        a, b = CHL[c]
+        out = A(("bt", "bl")[w], a, b)
+        if q == "s":
+            act(out, score(2 * c + w, b - a), ACT.Sign)
+        else:
+            ts(out, score(2 * c + w, b - a), 0.0, ALU.is_gt)
 
     for c in range(3):
         settle(0, c)
+    copy(A("glu", 0, 56), A("gli", 0, 56))
+    for r in range(1, 4):
+        copy(A("glu", 56, 112, p=(32 * r, 32 * r + 32)), A("gli", 56, 112, p=(32 * r - 32, 32 * r)))
+    copy(A("glu", 56, 112, p=g0), A("gli", 56, 112, p=(96, 112)))
+    signs(0, 0, "v")
+    signs(0, 1, "s")
+
     for s in STEPS:
         k = "%d" % s
-        xo, xn = "x%d" % (s - 1), "x" + k
-        qx, qxs = "qx%d" % (s - 1), "qxs%d" % (s - 1)
+        xo, xn, ko, kn = "x%d" % (s - 1), "x" + k, "k%d" % (s - 1), "k" + k
         first = s == 1
-        for a in range(0, 1792, 448):
-            spare.append(lambda a=a: ts(A("x64", a, a + 448), A(xo, a, a + 448), 64.0, ALU.mult))
-        if s < 3:
-            for a in range(0, C, PIECE):
-                spare.append(lambda a=a: join(s + 1, 0, a, a + PIECE))
+        ini = A("ini", 0, 1)
 
-        def host_gather(c, which):
+        def host(c, who):
             a, b = CHH[c]
-            for t in which:
-                copy(A("h" + k, 4 * a + t, 4 * b, 4), A(xo, by=A("hl", 28 * t + a // 16, 28 * t + b // 16)), "s")
+            for t in range(4):
+                if who[t] != "-":
+                    copy(A("h" + k, 4 * a + t, 4 * b, 4), A(xo, by=A("hl", 28 * t + a // 16, 28 * t + b // 16)), who[t])
 
         def host_send(c):
             a, b = CHH[c]
             quant(A("qh" + k, a, b), A("qhs" + k, a, b), A("h" + k, 4 * a, 4 * b))
-            sem = "c" + k + "ab"[c]
-            send(s, A("hc" + k, a, b, cast=dt.uint8), A("qh" + k, a, b, cast=dt.uint8), sem)
-            send(s, A("hcs" + k, a, b), A("qhs" + k, a, b), sem)
-            arrives(s, A("hc" + k, a, b), sem)
-            arrives(s, A("hcs" + k, a, b), sem)
+            send(s, [(A("hc" + k, a, b, cast=dt.uint8), A("qh" + k, a, b, cast=dt.uint8))], "c%d%d" % (s, c))
+            send(s, [(A("hcs" + k, a, b), A("qhs" + k, a, b))], "c%d%d" % (s, c))
 
-        def bits(n, c):
-            a, b = CHZ[c]
-            if n == 0:
-                ts(A("b2", a, b), score(c, b - a), 0.0, ALU.is_gt)
-            else:
-                ts(A("b1", a, b), score(3 + c, b - a), 0.0, ALU.is_gt, 2.0 ** -10, ALU.max)
-
-        for c, (a, b) in enumerate(CHZ):
-            mm(score(3 + c, b - a), A("qp", 128, 256), A("qps", 128, 256), A(qx, a, b), A(qxs, a, b))
-        if first:
-            host_gather(0, (0,))
-            nature(1, 0)
-            host_gather(0, (1, 2, 3))
-            nature(1, 1)
-        else:
-            host_gather(0, range(4))
-        host_gather(1, range(4))
-        for c in range(3):
-            bits(0, c)
-        if first:
-            join(1, 0, 0, 224)
-            join(1, 0, 224, 448)
-            bits(1, 0)
-        tt(A("t2"), A("b2", by=A("hx", 0, 28)), A("ea" + k), ALU.mult)
-        host_send(0)
-        scan(A("s2"), A("t2"))
-        if first:
-            bits(1, 1)
-            bits(1, 2)
-            even(1)
-        else:
-            bits(1, 0)
-        tt(A("lf"), wrapped("s2"), wrapped("gw"), ALU.add)
-        if first:
-            join(1, 1, 0, 224)
-        else:
-            bits(1, 1)
-        ts(A("l1"), A("lf"), 2 * BIG, ALU.add)
-        if first:
-            join(1, 1, 224, 448)
-            host_send(1)
-        else:
-            bits(1, 2)
-        tt(A("t1"), A("b1", by=A("hx", 28, 56)), A("eb" + k), ALU.mult)
-        copy(A("wb", 448, 896), A("wb", 0, 448, by=A("l1")), "s")
-        if first:
-            nature(2, 0)
-            gap()
-        else:
-            host_send(1)
-        ts(A("n1"), A("t1"), 1023, ALU.bitwise_and)
-        copy(A("l3", p=(0, 32)), A("l1", p=(0, 32)))
-        gap()
-        copy(A("wb", 896, 1344), A("n1", by=A("l1")))
-        copy(A("l3", p=(0, 16)), A("idl", p=(0, 16)))
-        gap()
-        scan(A("s3"), A("wb", 896, 1344))
-        gap()
-        ts(A("l2", p=(32, 64)), wrapped("s3", (0, 32)), BIG + 896.0, ALU.add)
-        ts(A("l2", p=(96, 128)), wrapped("s3", (64, 96)), A("off", p=(64, 96)), ALU.add)
-        ts(A("l3", p=(32, 64)), wrapped("s3", (0, 32)), A("off", p=(0, 32)), ALU.add)
-        if s < 3:
-            gap()
-        halves("wb", 1344, 1344, "l2")
-        gap()
-        scan(A("s4"), A("wb", 1344, 1792))
-        gap()
-        ts(A("l3", p=(64, 96)), wrapped("s4", (32, 64)), A("off", p=(32, 64)), ALU.add)
-        ts(A("l3", p=(96, 128)), wrapped("s4", (32, 64)), BIG + 1344.0, ALU.add)
-        gap()
-        halves("o5", 0, 1792, "l3")
-        if first:
-            nature(2, 1)
-            nature(3, 0)
-        elif s == 2:
-            nature(3, 1)
-        gap()
-        scan(A("s5"), A("o5"))
-        gap()
-        ts(A("vl" + k), wrapped("s5"), BIG, ALU.add)
-        send(s, A("vr" + k), A("vl" + k), "k" + k)
-        arrives(s, A("vr" + k), "k" + k)
-        gap(len(spare))
-        if s < 3:
-            even(s + 1)
-        for c, (a, b) in enumerate(CHH):
+        def unpack(c):
+            a, b = CHH[c]
             for t in range(4):
                 mm(bank(c, t, b - a), A("qe", 128 * t, 128 * t + 128), A("qes", 128 * t, 128 * t + 128), A("hc" + k, a, b), A("hcs" + k, a, b))
-            for t in range(4):
-                tt(A("m" + k, 448 * t + a, 448 * t + b), A(xo, 4 * a + t, 4 * b, 4), bank(c, t, b - a), ALU.max)
-            if s == 3 and c == 0:
-                copy(A("o8"), A("n1", by=A("vl" + k)))
-        if s == 3:
-            scan(A("s8"), A("o8"))
-            quant(A("qv"), A("qvs"), A("vt"))
-            ts(A("l8"), wrapped("s8"), BIG, ALU.add)
-            send(s, A("r8"), A("l8"), "k8")
-            arrives(s, A("r8"), "k8")
-        else:
-            join(s + 1, 1, 0, 224)
 
-        def mosaic(c, t, q):
-            a, b = CHZ[c]
-            copy(A("z" + k, 4 * a + t, 4 * b, 4), A("m" + k, 448 * t, 448 * t + 448, by=A("vr" + k, a // 16, b // 16)), q)
+        def larger(c, t):
+            a, b = CHH[c]
+            tt(A("m" + k, 448 * t + a, 448 * t + b), A(xo, 4 * a + t, 4 * b, 4), bank(c, t, b - a), ALU.max)
+
+        signs(1, 0, "v")
+        signs(1, 1, "s")
+        shared("at", 0, ("bt", 0, 448), "hu", 16, True)
+        shared("al", 0, ("bl", 0, 448), "hu", 8, True, 28)
+        scan(A("st"), A("at"), A("db"))
+        scan(A("sl"), A("al"), A("db"))
+        ts(A("it" + k), wrapped("st"), column(0), ALU.add)
+        tt(A("ib" + k), wrapped("sl"), A("kk"), ALU.add)
+        send(s, [(A("ir" + k), A("it" + k)), (A("br" + k), A("ib" + k))], "k" + k)
+        host(0, "sssv")
+        host(1, "---v")
+        host_send(0)
+        host(1, "ssv-")
+        host_send(1)
+        if first:
+            shared("gn", 0, ("idb", 0, 448), "glu", 20, False, 56, 56)
+            shared("gt", 0, ("idb", 0, 448), "glu", 0, False, 0, 56)
+            scan(A("s1"), A("gn", 0, 896, 2), A("db"))
+            scan(A("s2"), A("gn", 1, 896, 2), A("db"))
+            copy(A("dw"), A("pat", 16, 32, by=A("lw")))
+            tt(A("dl"), wrapped("s2"), wrapped("s1"), ALU.subtract)
+            tt(A("cl"), wrapped("s1"), A("kc"), ALU.add)
+            quant(A("qe"), A("qes"), A("ec"))
+            for a in range(0, 1792, 448):
+                spare.append(lambda a=a: ts(A(ko, a, a + 448), A(xo, a, a + 448), 64.0, ALU.mult))
+        if s == 1:
+            waits("y", A("hc1")[1], [])
+            dma("y", A("vt"), ext(T.v[:, :]), "dv")
+        if s == 3:
+            spare.append(lambda: quant(A("qv"), A("qvs"), A("vt")))
+        tt(A("la"), A("br" + k), A("dl"), ALU.mult)
+        shared("t0", 0, ("gt", 0, 896), "ir" + k, 10)
+        tt(A("lb"), A("la"), A("cl"), ALU.add)
+        gap()
+        copy(A("l1"), A("lb"))
+        gap()
+        shared("pw", 0, ("t0", 0, 448), "l1", 14)
+        scan(A("s1"), A("pw", 0, 448), A("dw"), ini)
+        gap()
+        ts(A("l2", p=(32, 64)), wrapped("s1", (0, 32)), column(1, (0, 32)), ALU.add)
+        ts(A("l2", p=(96, 128)), wrapped("s1", (64, 96)), BIG + MID, ALU.add)
+        shared("p2", 0, ("pw", 0, 448), "l2", 14)
+        unpack(0)
+        scan(A("s2"), A("p2"), A("dw"), ini)
+        gap()
+        ts(A("l3", p=(64, 96)), wrapped("s2", (32, 64)), BIG + MID, ALU.add)
+        ts(A("l3", p=(96, 128)), wrapped("s2", (32, 64)), BIG + MID, ALU.add)
+        shared("pw", 448, ("p2", 0, 448), "l3", 0)
+        unpack(1)
+        for t in range(4):
+            larger(0, t)
+        scan(A("s3"), A("pw", 448, 896), A("dw"), ini)
+        larger(1, 0)
+        ts(A("vl"), wrapped("s3"), column(1), ALU.add)
+        for t in range(1, 4):
+            larger(1, t)
+
+        def mosaic(c, who):
+            a, b = CH[c]
+            for t in range(4):
+                if who[t] != "-":
+                    copy(A("z" + k, 4 * a + t, 4 * b, 4), A("m" + k, 448 * t, 448 * t + 448, by=A("vl", a // 16, b // 16)), who[t])
 
         def layer(c):
-            a, b = CHZ[c]
+            a, b = CH[c]
             quant(A("qz" + k, a, b), A("qzs" + k, a, b), A("z" + k, 4 * a, 4 * b))
             for t in range(4):
                 mm(bank(c, t, b - a), A("qw", 128 * t, 128 * t + 128), A("qws", 128 * t, 128 * t + 128),
                    A("qz" + k, a, b), A("qzs" + k, a, b))
 
         def finish(c):
-            a, b = CHZ[c]
+            a, b = CH[c]
             for t in range(4):
-                tt(A("tmp", 448 * t + a, 448 * t + b), bank(c, t, b - a), A("x64", 4 * a + t, 4 * b, 4), ALU.add)
-                scaled(A(xn, 4 * a + t, 4 * b, 4), A("tmp", 448 * t + a, 448 * t + b), 2.0 ** -6)
+                tt(A(kn, 4 * a + t, 4 * b, 4), bank(c, t, b - a), A(ko, 4 * a + t, 4 * b, 4), ALU.add)
 
-        for c in range(3):
-            mosaic(c, 2, "s")
-            mosaic(c, 3, "s")
-        mosaic(2, 1, "s")
-        if s == 3:
-            copy(A("p7"), A("wb", 0, 448, by=A("vr3")), "s")
-            dma("y", ext(T.pl[0:7, :]), (T.p7[16:128:16, :], A("p7")[1]), "op_")
-        mosaic(0, 0, "v")
-        mosaic(0, 1, "v")
-        mosaic(1, 0, "v")
+        def shrink(c, q):
+            a, b = CH[c]
+            if q == "v":
+                ts(A(xn, 4 * a, 4 * b), A(kn, 4 * a, 4 * b), 2.0 ** -6, ALU.mult)
+            else:
+                act(A(xn, 4 * a, 4 * b), A(kn, 4 * a, 4 * b), scale=2.0 ** -6)
+
+        mosaic(0, "sssv")
+        mosaic(1, "---v")
         layer(0)
-        mosaic(1, 1, "v")
-        mosaic(2, 0, "v")
+        mosaic(1, "ssv-")
+        mosaic(2, "ssss")
+        if s == 3:
+            copy(A("l8", p=g0), A("vl", p=(96, 112)))
         layer(1)
         finish(0)
         layer(2)
+        shrink(0, "s")
         finish(1)
+        shrink(1, "s")
+        settle(s, 0)
         finish(2)
-        for c in range(3):
-            settle(s, c)
+        settle(s, 1)
+        shrink(2, "v")
+        settle(s, 2)
         if s < 3:
-            join(s + 1, 1, 224, 448)
+            signs(0, 0, "s")
+            signs(0, 1, "s")
 
-    for i in range(4):
-        dma("y", ext(T.osc[4 * i:4 * i + 4, :]), A("qxs3", p=(32 * i, 32 * i + 4)), "os_")
-    for c, (a, b) in enumerate(CHZ):
-        copy(A("yb", a, b), score(c, b - a), "ssv"[c])
+    act(A("p8"), A("pw", by=A("l8")), ACT.Identity, bias=MID)
+    for c, (a, b) in enumerate(CHL):
+        copy(A("yb", a, b), score(c, b - a), "sv"[c])
     dma("y", ext(T.y[:, :]), A("yb"), "oy")
-    copy(A("p8"), A("wb", 0, 448, by=A("r8")), "s")
-    dma("s", ext(T.pl[7:8, :]), A("p8", p=(112, 113)), "op_")
+    dma("s", ext(T.pl[0:7, :]), (T.p8[16:128:16, :], A("p8")[1]), "op_")
+    dma("s", ext(T.pl[7:8, :]), A("p8", p=(0, 1)), "op_")
+    for i in range(4):
+        dma("s", ext(T.osc[4 * i:4 * i + 4, :]), A("qxs3", p=(32 * i, 32 * i + 4)), "os_")
     for sem in sorted(total):
         if seen["p"].get(sem, 0) < total[sem]:
             g.wait_ge(T.sem[sem], total[sem])

@@ -28,7 +28,7 @@ _sbuf(BF, ut=512, vt=512, ec=2048, eye=128, pat=32, ini=2, idb=448, db=448, dw=4
 _sbuf(F16, st=448, sl=448, s1=448, s2=448, s3=448)
 _sbuf(F8, qu=128, qp=256, qv=128, qe=512, qw=512)
 _sbuf(U8, qus=128, qps=256, qvs=128, qes=512, qws=512)
-_sbuf(F32, cf=2, col=2, mm=16, e=16, ea=16, eb=16, i8=56, i32=28, kk=28, kc=28, dl=28, cl=28, la=28, lb=28, p8=448, yb=448)
+_sbuf(F32, cf=2, col=3, mm=16, e=16, ea=16, eb=16, i8=56, i32=28, kk=28, kc=28, dl=28, cl=28, la=28, lb=28, p8=448, yb=448)
 for _k in range(4):
     for _n, _w, _d in (("x", 1792, BF), ("k", 1792, BF), ("qx", 448, F8), ("qxs", 448, U8)):
         SCRATCH["%s%d" % (_n, _k)] = ("sbuf", [128, _w], _d)
@@ -37,9 +37,9 @@ for _k in STEPS:
                        ("qhs", 448, U8), ("hcs", 448, U8), ("qzs", 448, U8), ("it", 28, U16), ("ir", 28, U16),
                        ("ib", 28, BF), ("br", 28, BF)):
         SCRATCH["%s%d" % (_n, _k)] = ("sbuf", [128, _w], _d)
-SEMAPHORES = ["v", "s", "t", "p", "rl", "dgl", "dht", "dx0", "dx1", "dh2", "du", "dw", "dv", "oo", "os_", "oy", "op_"]
+SEMAPHORES = ["v", "s", "t", "p", "rl", "dgl", "dg2", "dht", "dx0", "dx1", "dh2", "du", "dw", "dv", "oo", "os_", "oy", "op_"]
 for _k in STEPS:
-    SEMAPHORES += ["k%d" % _k, "c%d0" % _k, "c%d1" % _k]
+    SEMAPHORES += ["j%d" % _k, "k%d" % _k, "c%d0" % _k, "c%d1" % _k]
 
 
 def rank_program(g, core, T, topo):
@@ -111,20 +111,14 @@ def rank_program(g, core, T, topo):
     def ext(view):
         return view, []
 
-    def send(step, moves, sem):
+    def send(step, out, in_, sem):
         dst = T.cores[rank ^ step]
         rid, pid, _ = topo.addr(dst)
-        eng = topo.engines(core, dst)
-        n = len(eng) // len(moves)
-        mv = []
-        for j, (out, in_) in enumerate(moves):
-            waits("p", in_[1], [])
-            mv.append(RemoteDMATransfer(dst_ids=[DstId(rid=rid, pnc=pid)], dma_engine_mask=sum(1 << e for e in eng[n * j:n * j + n]),
-                                        remote_sem=T.sem[sem], src=in_[0], dst=out[0]))
-            note([], out[1], sem, None)
-        g.remote_dma_fused(mv, local_sem=T.sem.rl)
-        total["rl"] = total.get("rl", 0) + len(eng)
+        waits("p", in_[1], [])
+        g.remote_dma(out[0], in_[0], T.sem[sem], T.sem.rl, pid, rid, topo.mask(core, dst))
+        total["rl"] = total.get("rl", 0) + len(topo.engines(core, dst))
         total[sem] = total.get(sem, 0) + len(topo.engines(dst, core))
+        note([], out[1], sem, None)
 
     def act(out, in_, func=ACT.Copy, **kw):
         run("s", lambda: g.scalar.activation(out[0], in_[0], func, **kw), [out], [in_])
@@ -176,7 +170,7 @@ def rank_program(g, core, T, topo):
         return A(("pa", "pb")[c % 2], 512 * t, 512 * t + n)
 
     def score(i, n):
-        return A("pb", 512 * i, 512 * i + n)
+        return A(("pb", "pa")[i // 4], 512 * (i % 4), 512 * (i % 4) + n)
 
     def shared(out, a, win, lst, cut, relu=False, base=0, n=28):
         for q, i, j in (("v", 0, cut), ("s", cut, n)):
@@ -205,8 +199,8 @@ def rank_program(g, core, T, topo):
     for c, (a, b) in enumerate(CHL):
         dma("y", A("x0", 4 * a, 4 * b), ext(T.x[:, 4 * a:4 * b]), "dx%d" % c)
     turned("s", "hti", 28, 28, T.ht, "dh2")
-    turned("y", "gli", 0, 56, T.gl, "dgl")
-    dma("y", A("gli", 56, 112), ext(T.gl[:, :]), "dgl")
+    turned("s", "gli", 0, 56, T.gl, "dgl")
+    dma("y", A("gli", 56, 112), ext(T.gl[:, :]), "dg2")
     waits("y", A("x0")[1], [])
     dma("y", A("qws"), ext(T.ws[:, :]), "dw")
     dma("y", A("qw", cast=dt.uint8), ext(T.wc[:, :]), "dw")
@@ -261,42 +255,46 @@ def rank_program(g, core, T, topo):
     ts(A("db", 15, 448, 16), A("i32"), A("pat", 15, 16), ALU.add)
     for t in range(4):
         copy(A("ec", 513 * t, 512 * t + 512, 4), A("eye"), "s")
-    ts(A("glu", 56, 112, p=(0, 32)), A("i8", p=(0, 32)), A("cf", 1, 2, p=(0, 32)), ALU.add)
-    ts(A("l2"), A("i8", 0, 28), 2.0, ALU.mult, i1, ALU.add)
-    ts(A("l3"), A("i8", 0, 28), 2.0, ALU.mult, i1, ALU.add)
-    ts(A("kc"), A("kk"), MID, ALU.add)
-    ts(A("l8"), A("l2"), 448.0, ALU.add)
-    copy(A("hu", 0, 28), A("hti", 28, 56))
+    copy(A("dw"), A("pat", 16, 32, by=A("lw")), "s")
 
     def settle(s, c):
         a, b = CH[c]
-        quant(A("qx%d" % s, a, b), A("qxs%d" % s, a, b), A("x%d" % s, 4 * a, 4 * b))
-        if c:
-            a, b = CHL[c - 1]
-            q, sc = A("qx%d" % s, a, b), A("qxs%d" % s, a, b)
-            if s < 3:
-                for w in range(2):
-                    mm(score(2 * c - 2 + w, b - a), A("qp", 128 * w, 128 * w + 128), A("qps", 128 * w, 128 * w + 128), q, sc)
-            else:
-                mm(score(c - 1, b - a), A("qv"), A("qvs"), q, sc)
+        q, sc = A("qx%d" % s, a, b), A("qxs%d" % s, a, b)
+        quant(q, sc, A("x%d" % s, 4 * a, 4 * b))
+        if s < 3:
+            for w in (1, 0):
+                mm(score(2 * c + w, b - a), A("qp", 128 * w, 128 * w + 128), A("qps", 128 * w, 128 * w + 128), q, sc)
+        else:
+            mm(score(c, b - a), A("qv"), A("qvs"), q, sc)
+            if c:
+                a, b = CHL[c - 1]
                 dma("y", ext(T.oc[:, 4 * a:4 * b]), A("qx3", a, b, cast=dt.uint8), "oo")
 
     def signs(c, w, q):
-        a, b = CHL[c]
+        a, b = CH[c]
         out = A(("bt", "bl")[w], a, b)
         if q == "s":
             act(out, score(2 * c + w, b - a), ACT.Sign)
         else:
             ts(out, score(2 * c + w, b - a), 0.0, ALU.is_gt)
 
+    def host(s, c, who, src):
+        a, b = CHH[c]
+        for t in range(4):
+            if who[t] != "-":
+                out, win = A("h%d" % s, 4 * a + t, 4 * b, 4), A(src, by=A("hl", 28 * t + a // 16, 28 * t + b // 16))
+                if src[0] == "k":
+                    act(out, win, scale=2.0 ** -6)
+                else:
+                    copy(out, win, who[t])
+
     for c in range(3):
         settle(0, c)
-    copy(A("glu", 0, 56), A("gli", 0, 56))
-    for r in range(1, 4):
-        copy(A("glu", 56, 112, p=(32 * r, 32 * r + 32)), A("gli", 56, 112, p=(32 * r - 32, 32 * r)))
-    copy(A("glu", 56, 112, p=g0), A("gli", 56, 112, p=(96, 112)))
-    signs(0, 0, "v")
-    signs(0, 1, "s")
+    copy(A("hu", 0, 28), A("hti", 28, 56))
+    host(1, 0, "ss--", "x0")
+    for c in range(2):
+        signs(c, 1, "v")
+        signs(c, 0, "v")
 
     for s in STEPS:
         k = "%d" % s
@@ -304,17 +302,11 @@ def rank_program(g, core, T, topo):
         first = s == 1
         ini = A("ini", 0, 1)
 
-        def host(c, who):
-            a, b = CHH[c]
-            for t in range(4):
-                if who[t] != "-":
-                    copy(A("h" + k, 4 * a + t, 4 * b, 4), A(xo, by=A("hl", 28 * t + a // 16, 28 * t + b // 16)), who[t])
-
         def host_send(c):
             a, b = CHH[c]
             quant(A("qh" + k, a, b), A("qhs" + k, a, b), A("h" + k, 4 * a, 4 * b))
-            send(s, [(A("hc" + k, a, b, cast=dt.uint8), A("qh" + k, a, b, cast=dt.uint8))], "c%d%d" % (s, c))
-            send(s, [(A("hcs" + k, a, b), A("qhs" + k, a, b))], "c%d%d" % (s, c))
+            send(s, A("hc" + k, a, b, cast=dt.uint8), A("qh" + k, a, b, cast=dt.uint8), "c%d%d" % (s, c))
+            send(s, A("hcs" + k, a, b), A("qhs" + k, a, b), "c%d%d" % (s, c))
 
         def unpack(c):
             a, b = CHH[c]
@@ -325,62 +317,75 @@ def rank_program(g, core, T, topo):
             a, b = CHH[c]
             tt(A("m" + k, 448 * t + a, 448 * t + b), A(xo, 4 * a + t, 4 * b, 4), bank(c, t, b - a), ALU.max)
 
-        signs(1, 0, "v")
-        signs(1, 1, "s")
-        shared("at", 0, ("bt", 0, 448), "hu", 16, True)
-        shared("al", 0, ("bl", 0, 448), "hu", 8, True, 28)
-        scan(A("st"), A("at"), A("db"))
+        signs(2, 1, "v")
+        signs(2, 0, "s")
+        shared("al", 0, ("bl", 0, 448), "hu", 14, True, 28)
+        shared("at", 0, ("bt", 0, 448), "hu", 14, True)
         scan(A("sl"), A("al"), A("db"))
-        ts(A("it" + k), wrapped("st"), column(0), ALU.add)
+        scan(A("st"), A("at"), A("db"))
         tt(A("ib" + k), wrapped("sl"), A("kk"), ALU.add)
-        send(s, [(A("ir" + k), A("it" + k)), (A("br" + k), A("ib" + k))], "k" + k)
-        host(0, "sssv")
-        host(1, "---v")
+        send(s, A("br" + k), A("ib" + k), "k" + k)
+        ts(A("it" + k), wrapped("st"), column(0), ALU.add)
+        send(s, A("ir" + k), A("it" + k), "j" + k)
+        if first:
+            copy(A("glu", 0, 56), A("gli", 0, 56))
+            ts(A("glu", 56, 112, p=(0, 32)), A("i8", p=(0, 32)), A("cf", 1, 2, p=(0, 32)), ALU.add)
+            for r in range(1, 4):
+                copy(A("glu", 56, 112, p=(32 * r, 32 * r + 32)), A("gli", 56, 112, p=(32 * r - 32, 32 * r)))
+            copy(A("glu", 56, 112, p=g0), A("gli", 56, 112, p=(96, 112)))
+            ts(A("l2"), A("i8", 0, 28), 2.0, ALU.mult, i1, ALU.add)
+            ts(A("l3"), A("i8", 0, 28), 2.0, ALU.mult, i1, ALU.add)
+            ts(A("kc"), A("kk"), MID, ALU.add)
+            ts(A("l8"), A("l2"), 448.0, ALU.add)
+        host(s, 0, "--sv" if first else "---s", xo)
+        host(s, 1, "---v", xo)
         host_send(0)
-        host(1, "ssv-")
+        host(s, 1, "sss-" if first else "ssv-", xo)
         host_send(1)
         if first:
             shared("gn", 0, ("idb", 0, 448), "glu", 20, False, 56, 56)
             shared("gt", 0, ("idb", 0, 448), "glu", 0, False, 0, 56)
+            quant(A("qe"), A("qes"), A("ec"))
             scan(A("s1"), A("gn", 0, 896, 2), A("db"))
             scan(A("s2"), A("gn", 1, 896, 2), A("db"))
-            copy(A("dw"), A("pat", 16, 32, by=A("lw")))
-            tt(A("dl"), wrapped("s2"), wrapped("s1"), ALU.subtract)
-            tt(A("cl"), wrapped("s1"), A("kc"), ALU.add)
-            quant(A("qe"), A("qes"), A("ec"))
             for a in range(0, 1792, 448):
                 spare.append(lambda a=a: ts(A(ko, a, a + 448), A(xo, a, a + 448), 64.0, ALU.mult))
-        if s == 1:
+            gap()
+            tt(A("dl"), wrapped("s2"), wrapped("s1"), ALU.subtract)
+            tt(A("cl"), wrapped("s1"), A("kc"), ALU.add)
             waits("y", A("hc1")[1], [])
             dma("y", A("vt"), ext(T.v[:, :]), "dv")
         if s == 3:
-            spare.append(lambda: quant(A("qv"), A("qvs"), A("vt")))
+            quant(A("qv"), A("qvs"), A("vt"))
         tt(A("la"), A("br" + k), A("dl"), ALU.mult)
-        shared("t0", 0, ("gt", 0, 896), "ir" + k, 10)
-        tt(A("lb"), A("la"), A("cl"), ALU.add)
         gap()
+        tt(A("lb"), A("la"), A("cl"), ALU.add)
+        shared("t0", 0, ("gt", 0, 896), "ir" + k, 12)
         copy(A("l1"), A("lb"))
         gap()
         shared("pw", 0, ("t0", 0, 448), "l1", 14)
-        scan(A("s1"), A("pw", 0, 448), A("dw"), ini)
         gap()
+        scan(A("s1"), A("pw", 0, 448), A("dw"), ini)
+        unpack(0)
+        unpack(1)
+        for c in range(2):
+            for t in range(4):
+                spare.append(lambda c=c, t=t: larger(c, t))
         ts(A("l2", p=(32, 64)), wrapped("s1", (0, 32)), column(1, (0, 32)), ALU.add)
         ts(A("l2", p=(96, 128)), wrapped("s1", (64, 96)), BIG + MID, ALU.add)
         shared("p2", 0, ("pw", 0, 448), "l2", 14)
-        unpack(0)
+        gap()
         scan(A("s2"), A("p2"), A("dw"), ini)
         gap()
         ts(A("l3", p=(64, 96)), wrapped("s2", (32, 64)), BIG + MID, ALU.add)
         ts(A("l3", p=(96, 128)), wrapped("s2", (32, 64)), BIG + MID, ALU.add)
-        shared("pw", 448, ("p2", 0, 448), "l3", 0)
-        unpack(1)
-        for t in range(4):
-            larger(0, t)
+        gap()
+        shared("pw", 448, ("p2", 0, 448), "l3", 14)
+        gap()
         scan(A("s3"), A("pw", 448, 896), A("dw"), ini)
-        larger(1, 0)
+        gap()
         ts(A("vl"), wrapped("s3"), column(1), ALU.add)
-        for t in range(1, 4):
-            larger(1, t)
+        gap(len(spare))
 
         def mosaic(c, who):
             a, b = CH[c]
@@ -405,13 +410,14 @@ def rank_program(g, core, T, topo):
             if q == "v":
                 ts(A(xn, 4 * a, 4 * b), A(kn, 4 * a, 4 * b), 2.0 ** -6, ALU.mult)
             else:
-                act(A(xn, 4 * a, 4 * b), A(kn, 4 * a, 4 * b), scale=2.0 ** -6)
+                for t in range(4):
+                    act(A(xn, 4 * a + t, 4 * b, 4), A(kn, 4 * a + t, 4 * b, 4), scale=2.0 ** -6)
 
-        mosaic(0, "sssv")
-        mosaic(1, "---v")
+        mosaic(0, "ssvs")
+        mosaic(1, "--vv")
         layer(0)
-        mosaic(1, "ssv-")
-        mosaic(2, "ssss")
+        mosaic(1, "ss--")
+        mosaic(2, "sssv")
         if s == 3:
             copy(A("l8", p=g0), A("vl", p=(96, 112)))
         layer(1)
@@ -422,19 +428,27 @@ def rank_program(g, core, T, topo):
         shrink(1, "s")
         settle(s, 0)
         finish(2)
+        if s < 3:
+            host(s + 1, 0, "sss-", kn)
+        else:
+            act(A("p8"), A("pw", by=A("l8")), ACT.Identity, bias=MID)
+            dma("s", ext(T.pl[0:7, :]), (T.p8[16:128:16, :], A("p8")[1]), "op_")
+            dma("s", ext(T.pl[7:8, :]), A("p8", p=(0, 1)), "op_")
         settle(s, 1)
         shrink(2, "v")
+        if s < 3:
+            signs(0, 1, "v")
+        else:
+            copy(A("yb", 0, 160), score(0, 160))
         settle(s, 2)
         if s < 3:
-            signs(0, 0, "s")
-            signs(0, 1, "s")
+            signs(1, 1, "v")
+            signs(0, 0, "v")
+            signs(1, 0, "v")
 
-    act(A("p8"), A("pw", by=A("l8")), ACT.Identity, bias=MID)
-    for c, (a, b) in enumerate(CHL):
-        copy(A("yb", a, b), score(c, b - a), "sv"[c])
+    copy(A("yb", 160, 320), score(1, 160))
+    copy(A("yb", 320, 448), score(2, 128))
     dma("y", ext(T.y[:, :]), A("yb"), "oy")
-    dma("s", ext(T.pl[0:7, :]), (T.p8[16:128:16, :], A("p8")[1]), "op_")
-    dma("s", ext(T.pl[7:8, :]), A("p8", p=(0, 1)), "op_")
     for i in range(4):
         dma("s", ext(T.osc[4 * i:4 * i + 4, :]), A("qxs3", p=(32 * i, 32 * i + 4)), "os_")
     for sem in sorted(total):

@@ -5,7 +5,7 @@ C = 448
 STEPS = (1, 2, 3)
 CH = ((0, 160), (160, 320), (320, 448))
 CHL = ((0, 320), (320, 448))
-CHH = ((0, 224), (224, 448))
+CHH = {1: ((0, 224), (224, 448)), 2: ((0, 160), (160, 448)), 3: ((0, 160), (160, 448))}
 BIG = 512.0
 MID = 224.0
 TOP = 240.0
@@ -47,7 +47,7 @@ def rank_program(g, core, T, topo):
     if rank is None:
         return
     queue = {"v": g.vector, "s": g.scalar, "t": g.tensor, "p": g, "y": g.sync}
-    total, log = {}, {}
+    total, log, known = {}, {}, {}
     seen = dict((q, {}) for q in queue)
 
     def A(name, a=0, b=None, step=1, p=None, cast=None, by=None):
@@ -83,6 +83,10 @@ def rank_program(g, core, T, topo):
                 for reg, was, sem, val in log.get(r[0], []):
                     if touch(r, reg) and (wr or was or r[0] in ("pa", "pb")):
                         need[sem] = max(need.get(sem, 0), total[sem] if val is None else val)
+        for sem in need:
+            for other, val in known.get((sem, need[sem]), {}).items():
+                if other != sem and seen[q].get(other, 0) < val:
+                    seen[q][other] = val
         for sem in sorted(need):
             if seen[q].get(sem, 0) < need[sem]:
                 queue[q].wait_ge(T.sem[sem], need[sem])
@@ -101,6 +105,7 @@ def rank_program(g, core, T, topo):
         call().then_inc(T.sem[q], 1)
         total[q] = total.get(q, 0) + 1
         note(reads, writes, q, total[q])
+        known[(q, total[q])] = dict(seen[q])
 
     def dma(q, out, in_, sem):
         waits(q, in_[1], out[1])
@@ -197,9 +202,9 @@ def rank_program(g, core, T, topo):
     dma("y", A("ut"), ext(T.u[:, :]), "du")
     dma("s", A("hti", 0, 28), ext(T.ht[:, :]), "dht")
     for c, (a, b) in enumerate(CHL):
-        dma("y", A("x0", 4 * a, 4 * b), ext(T.x[:, 4 * a:4 * b]), "dx%d" % c)
-    turned("s", "hti", 28, 28, T.ht, "dh2")
-    turned("s", "gli", 0, 56, T.gl, "dgl")
+        dma("sy"[c], A("x0", 4 * a, 4 * b), ext(T.x[:, 4 * a:4 * b]), "dx%d" % c)
+    turned("y", "hti", 28, 28, T.ht, "dh2")
+    turned("y", "gli", 0, 56, T.gl, "dgl")
     dma("y", A("gli", 56, 112), ext(T.gl[:, :]), "dg2")
     waits("y", A("x0")[1], [])
     dma("y", A("qws"), ext(T.ws[:, :]), "dw")
@@ -210,64 +215,72 @@ def rank_program(g, core, T, topo):
     iota(A("mm"), [[1, 16]], 0, 0)
     iota(A("uli"), [[-16, 2], [16, 8]], 112, 0, False)
     iota(A("i8"), [[8, 56]], 0, 0)
+    fill(A("ec", 0, 512), 0.0)
     fill(A("eye"), 1.0)
     iota(A("i32"), [[32, 28]], -1024, 0)
     run("p", lambda: g.affine_select(T.eye[:, :], T.eye[:, :], [[-1, 128]], ALU.is_equal, 0.0, 0, 1), [A("eye")], [A("eye")])
     iota(A("kk"), [[-32, 28]], 1536, 0)
     iota(A("idb"), [[1, 448]], -224, 0)
-    for k in range(4):
-        spare.append(lambda k=k: fill(A("ec", 512 * k, 512 * k + 512), 0.0))
-    gap()
+    for k in range(1, 4):
+        copy(A("ec", 512 * k, 512 * k + 512), A("ec", 0, 512), "s")
     ts(A("ci", 0, 1), A("pi"), 15, ALU.bitwise_and)
     ts(A("ci", 1, 2), A("pi"), 15, ALU.bitwise_and, 1, ALU.logical_shift_right)
     fill(A("ini"), -BIG)
     fill(column(1), BIG + MID)
+    ts(A("ulm"), A("uli"), 127, ALU.bitwise_and)
     copy(A("cf"), A("ci"))
     fill(column(1, g0), -TOP)
-    ts(A("ulm"), A("uli"), 127, ALU.bitwise_and)
+    copy(A("ul"), A("ulm"))
     i1 = A("cf", 0, 1)
     ts(A("e"), A("mm"), i1, ALU.subtract)
     ts(A("lw"), A("i8", 0, 28), 0.0, ALU.mult, i1, ALU.add)
-    copy(A("ul"), A("ulm"))
-    ts(A("ea"), A("e"), 0.0, ALU.is_equal, BIG, ALU.mult)
-    ts(A("eb"), A("e"), 0.0, ALU.is_lt, -BIG, ALU.mult)
-    gap()
-    tt(A("e"), A("ea"), A("eb"), ALU.add)
     ts(column(0), i1, 2.0, ALU.mult, 3 * BIG, ALU.add)
     ts(A("ini", 0, 1, p=g0), A("cf", 0, 1, p=g0), TOP - 16, ALU.add)
-    ts(A("e", 15, 16), A("e", 15, 16), -2 * BIG, ALU.add)
-    gap()
-    copy(A("pat", 0, 16), A("e"))
-    copy(A("pat", 16, 32), A("e"))
-    gap()
-    copy(A("db"), A("pat", 0, 16, by=A("lw")), "s")
-    fill(A("pat", 16, 32, p=g0), 0.0)
-    for t in range(4):
+    ts(A("ea"), A("e"), 0.0, ALU.is_equal, BIG, ALU.mult)
+    ts(A("eb"), A("e"), 0.0, ALU.is_lt, -BIG, ALU.mult)
+    ts(A("l2"), A("i8", 0, 28), 2.0, ALU.mult, i1, ALU.add)
+    ts(A("l3"), A("i8", 0, 28), 2.0, ALU.mult, i1, ALU.add)
+    ts(A("glu", 56, 112, p=(0, 32)), A("i8", p=(0, 32)), A("cf", 1, 2, p=(0, 32)), ALU.add)
+    tt(A("pat", 0, 16), A("ea"), A("eb"), ALU.add)
+    tt(A("pat", 16, 32), A("ea"), A("eb"), ALU.add)
+    ts(A("l8"), A("l2"), 448.0, ALU.add)
+    for t in range(2):
         ts(A("hl", 28 * t, 28 * t + 28), A("hti", 0, 28), 4.0, ALU.mult, float(t), ALU.add)
-    fill(A("pat", 16, 17, p=g0), 16.0)
+    copy(A("db"), A("pat", 0, 16, by=A("lw")), "s")
+    ts(column(2), A("pat", 15, 16), -2 * BIG, ALU.add)
+    ts(A("pat", 31, 32), A("pat", 15, 16), -2 * BIG, ALU.add)
     quant(A("qu"), A("qus"), A("ut"))
-    for r in range(4):
-        q = (r - 1) % 4
-        copy(A("hu", 28, 56, p=(32 * r, 32 * r + 32)), A("hti", 0, 28, p=(32 * q, 32 * q + 32)))
+    for t in range(2, 4):
+        ts(A("hl", 28 * t, 28 * t + 28), A("hti", 0, 28), 4.0, ALU.mult, float(t), ALU.add)
+    fill(A("pat", 16, 32, p=g0), 0.0)
+    ts(A("kc"), A("kk"), MID, ALU.add)
     ul = A("ul")
     copy(A("qps"), A("qus", by=ul), "s")
     copy(A("qp", cast=dt.uint32), A("qu", cast=dt.uint32, by=ul))
-    ts(A("db", 15, 448, 16), A("i32"), A("pat", 15, 16), ALU.add)
+    fill(A("pat", 16, 17, p=g0), 16.0)
+    for r in range(4):
+        q = (r - 1) % 4
+        copy(A("hu", 28, 56, p=(32 * r, 32 * r + 32)), A("hti", 0, 28, p=(32 * q, 32 * q + 32)))
     for t in range(4):
         copy(A("ec", 513 * t, 512 * t + 512, 4), A("eye"), "s")
     copy(A("dw"), A("pat", 16, 32, by=A("lw")), "s")
 
-    def settle(s, c):
+    def scores(s, c, w):
+        a, b = CH[c]
+        mm(score(2 * c + w, b - a), A("qp", 128 * w, 128 * w + 128), A("qps", 128 * w, 128 * w + 128),
+           A("qx%d" % s, a, b), A("qxs%d" % s, a, b))
+
+    def settle(s, c, sides=(1, 0)):
         a, b = CH[c]
         q, sc = A("qx%d" % s, a, b), A("qxs%d" % s, a, b)
         quant(q, sc, A("x%d" % s, 4 * a, 4 * b))
         if s < 3:
-            for w in (1, 0):
-                mm(score(2 * c + w, b - a), A("qp", 128 * w, 128 * w + 128), A("qps", 128 * w, 128 * w + 128), q, sc)
+            for w in sides:
+                scores(s, c, w)
         else:
             mm(score(c, b - a), A("qv"), A("qvs"), q, sc)
-            if c:
-                a, b = CHL[c - 1]
+            if c != 1:
+                a = CH[c // 2][0]
                 dma("y", ext(T.oc[:, 4 * a:4 * b]), A("qx3", a, b, cast=dt.uint8), "oo")
 
     def signs(c, w, q):
@@ -279,7 +292,7 @@ def rank_program(g, core, T, topo):
             ts(out, score(2 * c + w, b - a), 0.0, ALU.is_gt)
 
     def host(s, c, who, src):
-        a, b = CHH[c]
+        a, b = CHH[s][c]
         for t in range(4):
             if who[t] != "-":
                 out, win = A("h%d" % s, 4 * a + t, 4 * b, 4), A(src, by=A("hl", 28 * t + a // 16, 28 * t + b // 16))
@@ -288,13 +301,15 @@ def rank_program(g, core, T, topo):
                 else:
                     copy(out, win, who[t])
 
-    for c in range(3):
-        settle(0, c)
-    copy(A("hu", 0, 28), A("hti", 28, 56))
+    settle(0, 0)
+    settle(0, 1)
+    ts(A("db", 15, 448, 16), A("i32"), column(2), ALU.add)
+    settle(0, 2)
     host(1, 0, "ss--", "x0")
     for c in range(2):
         signs(c, 1, "v")
         signs(c, 0, "v")
+    copy(A("hu", 0, 28), A("hti", 28, 56))
 
     for s in STEPS:
         k = "%d" % s
@@ -302,53 +317,60 @@ def rank_program(g, core, T, topo):
         first = s == 1
         ini = A("ini", 0, 1)
 
-        def host_send(c):
-            a, b = CHH[c]
+        def codes(c):
+            a, b = CHH[s][c]
             quant(A("qh" + k, a, b), A("qhs" + k, a, b), A("h" + k, 4 * a, 4 * b))
             send(s, A("hc" + k, a, b, cast=dt.uint8), A("qh" + k, a, b, cast=dt.uint8), "c%d%d" % (s, c))
+
+        def scales(c):
+            a, b = CHH[s][c]
             send(s, A("hcs" + k, a, b), A("qhs" + k, a, b), "c%d%d" % (s, c))
 
         def unpack(c):
-            a, b = CHH[c]
+            a, b = CHH[s][c]
             for t in range(4):
                 mm(bank(c, t, b - a), A("qe", 128 * t, 128 * t + 128), A("qes", 128 * t, 128 * t + 128), A("hc" + k, a, b), A("hcs" + k, a, b))
 
         def larger(c, t):
-            a, b = CHH[c]
+            a, b = CHH[s][c]
             tt(A("m" + k, 448 * t + a, 448 * t + b), A(xo, 4 * a + t, 4 * b, 4), bank(c, t, b - a), ALU.max)
 
         signs(2, 1, "v")
-        signs(2, 0, "s")
-        shared("al", 0, ("bl", 0, 448), "hu", 14, True, 28)
+        if first:
+            signs(2, 0, "s")
+            for r in range(1, 4):
+                copy(A("glu", 56, 112, p=(32 * r, 32 * r + 32)), A("gli", 56, 112, p=(32 * r - 32, 32 * r)))
+            copy(A("glu", 56, 112, p=g0), A("gli", 56, 112, p=(96, 112)))
+        else:
+            signs(1, 0, "s")
+            signs(2, 0, "v")
+            codes(0)
+        shared("al", 0, ("bl", 0, 448), "hu", 14 if first else 10, True, 28)
         shared("at", 0, ("bt", 0, 448), "hu", 14, True)
         scan(A("sl"), A("al"), A("db"))
         scan(A("st"), A("at"), A("db"))
         tt(A("ib" + k), wrapped("sl"), A("kk"), ALU.add)
         send(s, A("br" + k), A("ib" + k), "k" + k)
+        if first:
+            copy(A("glu", 0, 56), A("gli", 0, 56))
         ts(A("it" + k), wrapped("st"), column(0), ALU.add)
         send(s, A("ir" + k), A("it" + k), "j" + k)
         if first:
-            copy(A("glu", 0, 56), A("gli", 0, 56))
-            ts(A("glu", 56, 112, p=(0, 32)), A("i8", p=(0, 32)), A("cf", 1, 2, p=(0, 32)), ALU.add)
-            for r in range(1, 4):
-                copy(A("glu", 56, 112, p=(32 * r, 32 * r + 32)), A("gli", 56, 112, p=(32 * r - 32, 32 * r)))
-            copy(A("glu", 56, 112, p=g0), A("gli", 56, 112, p=(96, 112)))
-            ts(A("l2"), A("i8", 0, 28), 2.0, ALU.mult, i1, ALU.add)
-            ts(A("l3"), A("i8", 0, 28), 2.0, ALU.mult, i1, ALU.add)
-            ts(A("kc"), A("kk"), MID, ALU.add)
-            ts(A("l8"), A("l2"), 448.0, ALU.add)
-        host(s, 0, "--sv" if first else "---s", xo)
-        host(s, 1, "---v", xo)
-        host_send(0)
-        host(s, 1, "sss-" if first else "ssv-", xo)
-        host_send(1)
+            host(s, 0, "--sv", xo)
+            host(s, 1, "---v", xo)
+            codes(0)
+        scales(0)
+        host(s, 1, "sss-" if first else "ssvv", xo)
+        codes(1)
+        scales(1)
         if first:
             shared("gn", 0, ("idb", 0, 448), "glu", 20, False, 56, 56)
-            shared("gt", 0, ("idb", 0, 448), "glu", 0, False, 0, 56)
-            quant(A("qe"), A("qes"), A("ec"))
+            shared("gt", 0, ("idb", 0, 448), "glu", 12, False, 0, 56)
             scan(A("s1"), A("gn", 0, 896, 2), A("db"))
             scan(A("s2"), A("gn", 1, 896, 2), A("db"))
-            for a in range(0, 1792, 448):
+            for a in (0, 256):
+                spare.append(lambda a=a: quant(A("qe", a, a + 256), A("qes", a, a + 256), A("ec", 4 * a, 4 * a + 1024)))
+            for a in (0, 448):
                 spare.append(lambda a=a: ts(A(ko, a, a + 448), A(xo, a, a + 448), 64.0, ALU.mult))
             gap()
             tt(A("dl"), wrapped("s2"), wrapped("s1"), ALU.subtract)
@@ -364,6 +386,8 @@ def rank_program(g, core, T, topo):
         copy(A("l1"), A("lb"))
         gap()
         shared("pw", 0, ("t0", 0, 448), "l1", 14)
+        if first:
+            act(A(ko, 896, 1792), A(xo, 896, 1792), scale=64.0)
         gap()
         scan(A("s1"), A("pw", 0, 448), A("dw"), ini)
         unpack(0)
@@ -371,12 +395,15 @@ def rank_program(g, core, T, topo):
         for c in range(2):
             for t in range(4):
                 spare.append(lambda c=c, t=t: larger(c, t))
+        early = int(not first)
+        gap(early)
         ts(A("l2", p=(32, 64)), wrapped("s1", (0, 32)), column(1, (0, 32)), ALU.add)
         ts(A("l2", p=(96, 128)), wrapped("s1", (64, 96)), BIG + MID, ALU.add)
+        gap(early)
         shared("p2", 0, ("pw", 0, 448), "l2", 14)
         gap()
         scan(A("s2"), A("p2"), A("dw"), ini)
-        gap()
+        gap(1 - early)
         ts(A("l3", p=(64, 96)), wrapped("s2", (32, 64)), BIG + MID, ALU.add)
         ts(A("l3", p=(96, 128)), wrapped("s2", (32, 64)), BIG + MID, ALU.add)
         gap()
@@ -426,31 +453,29 @@ def rank_program(g, core, T, topo):
         shrink(0, "s")
         finish(1)
         shrink(1, "s")
-        settle(s, 0)
         finish(2)
+        settle(s, 0)
         if s < 3:
-            host(s + 1, 0, "sss-", kn)
+            host(s + 1, 0, "ssss", kn)
         else:
             act(A("p8"), A("pw", by=A("l8")), ACT.Identity, bias=MID)
             dma("s", ext(T.pl[0:7, :]), (T.p8[16:128:16, :], A("p8")[1]), "op_")
             dma("s", ext(T.pl[7:8, :]), A("p8", p=(0, 1)), "op_")
-        settle(s, 1)
         shrink(2, "v")
+        settle(s, 1, (1,))
+        settle(s, 2, (1,))
         if s < 3:
+            scores(s, 1, 0)
+            scores(s, 2, 0)
             signs(0, 1, "v")
-        else:
-            copy(A("yb", 0, 160), score(0, 160))
-        settle(s, 2)
-        if s < 3:
-            signs(1, 1, "v")
             signs(0, 0, "v")
-            signs(1, 0, "v")
+            signs(1, 1, "v")
 
-    copy(A("yb", 160, 320), score(1, 160))
-    copy(A("yb", 320, 448), score(2, 128))
+    for c, (a, b) in enumerate(CH):
+        copy(A("yb", a, b), score(c, b - a))
     dma("y", ext(T.y[:, :]), A("yb"), "oy")
     for i in range(4):
         dma("s", ext(T.osc[4 * i:4 * i + 4, :]), A("qxs3", p=(32 * i, 32 * i + 4)), "os_")
     for sem in sorted(total):
-        if seen["p"].get(sem, 0) < total[sem]:
-            g.wait_ge(T.sem[sem], total[sem])
+        if max(seen[q].get(sem, 0) for q in queue) < total[sem]:
+            queue[{"oo": "y", "oy": "y", "op_": "s", "os_": "s"}.get(sem, "p")].wait_ge(T.sem[sem], total[sem])

@@ -5,7 +5,7 @@ C = 448
 STEPS = (1, 2, 3)
 CH = ((0, 160), (160, 320), (320, 448))
 CHL = ((0, 320), (320, 448))
-CHH = {1: ((0, 224), (224, 448)), 2: ((0, 160), (160, 448)), 3: ((0, 160), (160, 448))}
+CHH = dict((_s, ((0, 128), (128, 288), (288, 448))) for _s in STEPS)
 BIG = 512.0
 MID = 224.0
 TOP = 240.0
@@ -21,25 +21,25 @@ def _sbuf(kind, **widths):
         SCRATCH[name] = ("sbuf", [128, widths[name]], kind)
 
 
-_sbuf(I32, gli=112, hti=56, uli=16, ulm=16, pi=1, ci=2)
-_sbuf(U16, glu=112, hu=56, hl=112, ul=16, lw=28, l1=28, l2=28, l3=28, vl=28, l8=28)
-_sbuf(BF, ut=512, vt=512, ec=2048, eye=128, pat=32, ini=2, idb=448, db=448, dw=448, gt=896, gn=896, bt=448, bl=448,
-      at=448, al=448, t0=448, pw=896, p2=448)
+_sbuf(I32, gli=112, hti=84, uli=9)
+_sbuf(U16, glu=56, shl=4, hu=56, hl=112, ul=9, lw=28, l1=28, l2=28, l3=28, l4=14, vl=28)
+_sbuf(BF, ut=512, vt=512, ec=516, one=128, pat=32, ini=2, ib=168, idb=448, db=448, dw=448, dz=224, gt=896, bt=448, bl=448,
+      at=448, al=448, t0=448, p1=448, p2=896, p3=448)
 _sbuf(F16, st=448, sl=448, s1=448, s2=448, s3=448)
-_sbuf(F8, qu=128, qp=256, qv=128, qe=512, qw=512)
-_sbuf(U8, qus=128, qps=256, qvs=128, qes=512, qws=512)
-_sbuf(F32, cf=2, col=3, mm=16, e=16, ea=16, eb=16, i8=56, i32=28, kk=28, kc=28, dl=28, cl=28, la=28, lb=28, p8=448, yb=448)
+_sbuf(F8, qu=128, qp=144, qv=128, qe=512, qw=512)
+_sbuf(U8, qus=128, qps=144, qvs=128, qes=512, qws=512)
+_sbuf(F32, col=2, sh=4, nn=96, nt=96, e=32, ea=32, eb=32, i8=56, i32=28, kk=28, g1=64, g2=64, g3=64, g4=64, dc=56, la=56,
+      p8=448, yb=448)
 for _k in range(4):
     for _n, _w, _d in (("x", 1792, BF), ("k", 1792, BF), ("qx", 448, F8), ("qxs", 448, U8)):
         SCRATCH["%s%d" % (_n, _k)] = ("sbuf", [128, _w], _d)
 for _k in STEPS:
     for _n, _w, _d in (("h", 1792, BF), ("m", 1792, BF), ("z", 1792, BF), ("qh", 448, F8), ("hc", 448, F8), ("qz", 448, F8),
-                       ("qhs", 448, U8), ("hcs", 448, U8), ("qzs", 448, U8), ("it", 28, U16), ("ir", 28, U16),
-                       ("ib", 28, BF), ("br", 28, BF)):
+                       ("qhs", 448, U8), ("hcs", 448, U8), ("qzs", 448, U8), ("it", 28, U16), ("ir", 28, U16), ("br", 56, BF)):
         SCRATCH["%s%d" % (_n, _k)] = ("sbuf", [128, _w], _d)
 SEMAPHORES = ["v", "s", "t", "p", "rl", "dgl", "dg2", "dht", "dx0", "dx1", "dh2", "du", "dw", "dv", "oo", "os_", "oy", "op_"]
 for _k in STEPS:
-    SEMAPHORES += ["j%d" % _k, "k%d" % _k, "c%d0" % _k, "c%d1" % _k]
+    SEMAPHORES += ["j%d" % _k, "k%d" % _k, "c%d0" % _k, "c%d1" % _k, "c%d2" % _k]
 
 
 def rank_program(g, core, T, topo):
@@ -142,11 +142,20 @@ def rank_program(g, core, T, topo):
         else:
             run("v", lambda: g.vector.tensor_scalar(out[0], in_[0], a0, b0, op0, op1), [out], [in_] + col)
 
+    def times(out, in_, c, q):
+        if q == "v":
+            ts(out, in_, c, ALU.mult)
+        else:
+            act(out, in_, scale=c)
+
     def tt(out, a, b, op):
         run("v", lambda: g.vector.tensor_tensor(out[0], a[0], b[0], op), [out], [a, b])
 
     def fill(out, c):
         run("v", lambda: g.vector.memset(out[0], c), [out], [])
+
+    def turn(out, in_):
+        run("v", lambda: g.vector.transpose(out[0], in_[0]), [out], [in_])
 
     def quant(q, s, in_):
         run("v", lambda: g.vector.quantize_mx(q[0], s[0], in_[0]), [q, s], [in_])
@@ -154,19 +163,19 @@ def rank_program(g, core, T, topo):
     def mm(out, l, ls, r, rs):
         run("t", lambda: g.tensor.matmul_mx(out[0], l[0], ls[0], r[0], rs[0], True, True), [out], [l, ls, r, rs])
 
-    def iota(out, pattern, base, cm, f=True):
+    def iota(out, pattern, base, f=True):
         if f:
-            run("p", lambda: g.iota(out[0], pattern, base, cm, allow_small_or_imprecise_dtypes=True), [out], [])
+            run("p", lambda: g.iota(out[0], pattern, base, 0, allow_small_or_imprecise_dtypes=True), [out], [])
         else:
-            run("p", lambda: g.iota(out[0], pattern, base, cm), [out], [])
+            run("p", lambda: g.iota(out[0], pattern, base, 0), [out], [])
 
-    def scan(out, in_, d, first=-BIG):
+    def scan(out, in_, d, first=-BIG, op=ALU.max):
         col = [first] if isinstance(first, tuple) else []
         f0 = first[0] if col else first
-        run("v", lambda: g.vector.tensor_tensor_scan(out[0], in_[0], d[0], f0, ALU.max, ALU.add), [out], [in_, d] + col)
+        run("v", lambda: g.vector.tensor_tensor_scan(out[0], in_[0], d[0], f0, op, ALU.add), [out], [in_, d] + col)
 
-    def wrapped(name, p=None):
-        return A(name, 15, 448, 16, p)
+    def wrapped(name, p=None, a=0, b=448):
+        return A(name, a + 15, b, 16, p)
 
     def column(i, p=None):
         return A("col", i, i + 1, p=p)
@@ -177,113 +186,94 @@ def rank_program(g, core, T, topo):
     def score(i, n):
         return A(("pb", "pa")[i // 4], 512 * (i % 4), 512 * (i % 4) + n)
 
-    def shared(out, a, win, lst, cut, relu=False, base=0, n=28):
-        for q, i, j in (("v", 0, cut), ("s", cut, n)):
-            if i < j:
-                o, w = A(out, a + 16 * i, a + 16 * j), A(win[0], win[1], win[2], by=A(lst, base + i, base + j))
-                if not relu:
-                    copy(o, w, q)
-                elif q == "v":
-                    ts(o, w, 0.0, ALU.max)
-                else:
-                    act(o, w, ACT.Relu)
+    def shared(out, win, lst, cut, relu=False, base=0):
+        for q, i, j in (("v", 0, cut), ("s", cut, 28)):
+            o, w = A(out, 16 * i, 16 * j), A(win, 0, 896 if win == "gt" else 448, by=A(lst, base + i, base + j))
+            if not relu:
+                copy(o, w, q)
+            elif q == "v":
+                ts(o, w, 0.0, ALU.max)
+            else:
+                act(o, w, ACT.Relu)
 
-    spare = []
+    def turned(name, a, w, src, n, sem):
+        dma("y", A(name, a, a + w, p=(n, 128)), ext(src[0:128 - n, :]), sem)
+        dma("y", A(name, a, a + w, p=(0, n)), ext(src[128 - n:128, :]), sem)
 
-    def gap(n=1):
-        while n and spare:
-            spare.pop(0)()
-            n -= 1
-
-    def turned(q, name, a, w, src, sem):
-        dma(q, A(name, a, a + w, p=(16, 128)), ext(src[0:112, :]), sem)
-        dma(q, A(name, a, a + w, p=(0, 16)), ext(src[112:128, :]), sem)
-
+    g0, low, high = (0, 16), (0, 64), (64, 128)
     dma("y", A("ut"), ext(T.u[:, :]), "du")
     dma("s", A("hti", 0, 28), ext(T.ht[:, :]), "dht")
     for c, (a, b) in enumerate(CHL):
         dma("sy"[c], A("x0", 4 * a, 4 * b), ext(T.x[:, 4 * a:4 * b]), "dx%d" % c)
-    turned("y", "hti", 28, 28, T.ht, "dh2")
-    turned("y", "gli", 0, 56, T.gl, "dgl")
-    dma("y", A("gli", 56, 112), ext(T.gl[:, :]), "dg2")
+    turned("gli", 56, 56, T.gl, 16, "dgl")
+    turned("hti", 56, 28, T.ht, 32, "dh2")
+    turned("hti", 28, 28, T.ht, 16, "dh2")
+
+    iota(A("nn", 0, 32), [[0, 2], [1, 16]], 0)
+    iota(A("nn", 32, 64), [[0, 2], [1, 8], [0, 2]], 0)
+    iota(A("uli", 0, 2), [[16, 2]], 96, False)
+    iota(A("uli", 2, 9), [[16, 7]], 0, False)
+    iota(A("i8"), [[8, 56]], 0)
+    fill(A("ec"), 0.0)
+    fill(A("one"), 1.0)
+    turn(A("nt", 0, 32), A("nn", 0, 32))
+    i1 = A("nt", 0, 1)
+    fill(column(1), BIG + MID)
+    fill(A("ini"), -BIG)
+    tt(A("e"), A("nn", 0, 32), A("nt", 0, 32), ALU.subtract)
+    act(column(0), i1, ACT.Identity, scale=2.0, bias=3 * BIG)
+    act(A("ini", 0, 1, p=g0), A("nt", 0, 1, p=g0), ACT.Identity, bias=TOP - 16)
+    act(column(1, g0), A("nn", 0, 1, p=g0), ACT.Identity, bias=-TOP)
+    fill(A("ib"), 0.0)
+    ts(A("eb"), A("e"), 0.0, ALU.is_lt, -BIG, ALU.mult)
+    ts(A("ea"), A("e"), 0.0, ALU.is_equal, BIG, ALU.mult)
+    eye = A("ec", 3, 515, 4)
+    run("p", lambda: g.affine_select(eye[0], T.one[:, :], [[-1, 128]], ALU.is_equal, 0.0, 0, 1), [eye], [A("one")])
+    iota(A("nn", 64, 96), [[0, 2], [32, 2], [2, 8]], 0)
+    iota(A("i32"), [[32, 28]], -1024)
+    iota(A("idb"), [[1, 448]], -224)
+    iota(A("sh"), [[1, 2], [16, 2]], 0)
+    iota(A("kk"), [[-32, 28]], 1536)
+    copy(A("ul"), A("uli"))
+    tt(A("pat"), A("ea"), A("eb"), ALU.add)
+    ts(A("lw"), A("i8", 0, 28), 0.0, ALU.mult, i1, ALU.add)
+    ts(A("l2"), A("i8", 0, 28), 2.0, ALU.mult, i1, ALU.add)
+    ts(A("pat", 15, 32, 16), A("pat", 15, 32, 16), -2 * BIG, ALU.add)
+    copy(A("db"), A("pat", 0, 16, by=A("lw")), "s")
+    ini, ul = A("ini", 0, 1), A("ul")
+    quant(A("qu"), A("qus"), A("ut"))
+    copy(A("qps"), A("qus", by=ul), "s")
+    for t in range(4):
+        ts(A("hl", 28 * t, 28 * t + 28), A("hti", 0, 28), 4.0, ALU.mult, float(t), ALU.add)
+    copy(A("qp", cast=dt.uint32), A("qu", cast=dt.uint32, by=ul))
+    turn(A("nt", 32, 96), A("nn", 32, 96))
+    ts(A("gli", 0, 56, p=(0, 32)), A("i8", p=(0, 32)), A("nt", 32, 33, p=(0, 32)), ALU.add)
+    dma("y", A("gli", 0, 56, p=(32, 128)), ext(T.gl[0:96, :]), "dg2")
+    dma("y", A("gli", 0, 56, p=g0), ext(T.gl[96:112, :]), "dg2")
     waits("y", A("x0")[1], [])
     dma("y", A("qws"), ext(T.ws[:, :]), "dw")
     dma("y", A("qw", cast=dt.uint8), ext(T.wc[:, :]), "dw")
+    ts(A("pat", 16, 32, p=g0), A("nn", 0, 16, p=g0), 0.0, ALU.is_equal, 16.0, ALU.mult)
 
-    g0 = (0, 16)
-    iota(A("pi"), [[0, 1]], 0, 1, False)
-    iota(A("mm"), [[1, 16]], 0, 0)
-    iota(A("uli"), [[-16, 2], [16, 8]], 112, 0, False)
-    iota(A("i8"), [[8, 56]], 0, 0)
-    fill(A("ec", 0, 512), 0.0)
-    fill(A("eye"), 1.0)
-    iota(A("i32"), [[32, 28]], -1024, 0)
-    run("p", lambda: g.affine_select(T.eye[:, :], T.eye[:, :], [[-1, 128]], ALU.is_equal, 0.0, 0, 1), [A("eye")], [A("eye")])
-    iota(A("kk"), [[-32, 28]], 1536, 0)
-    iota(A("idb"), [[1, 448]], -224, 0)
-    for k in range(1, 4):
-        copy(A("ec", 512 * k, 512 * k + 512), A("ec", 0, 512), "s")
-    ts(A("ci", 0, 1), A("pi"), 15, ALU.bitwise_and)
-    ts(A("ci", 1, 2), A("pi"), 15, ALU.bitwise_and, 1, ALU.logical_shift_right)
-    fill(A("ini"), -BIG)
-    fill(column(1), BIG + MID)
-    ts(A("ulm"), A("uli"), 127, ALU.bitwise_and)
-    copy(A("cf"), A("ci"))
-    fill(column(1, g0), -TOP)
-    copy(A("ul"), A("ulm"))
-    i1 = A("cf", 0, 1)
-    ts(A("e"), A("mm"), i1, ALU.subtract)
-    ts(A("lw"), A("i8", 0, 28), 0.0, ALU.mult, i1, ALU.add)
-    ts(column(0), i1, 2.0, ALU.mult, 3 * BIG, ALU.add)
-    ts(A("ini", 0, 1, p=g0), A("cf", 0, 1, p=g0), TOP - 16, ALU.add)
-    ts(A("ea"), A("e"), 0.0, ALU.is_equal, BIG, ALU.mult)
-    ts(A("eb"), A("e"), 0.0, ALU.is_lt, -BIG, ALU.mult)
-    ts(A("l2"), A("i8", 0, 28), 2.0, ALU.mult, i1, ALU.add)
-    ts(A("l3"), A("i8", 0, 28), 2.0, ALU.mult, i1, ALU.add)
-    ts(A("glu", 56, 112, p=(0, 32)), A("i8", p=(0, 32)), A("cf", 1, 2, p=(0, 32)), ALU.add)
-    tt(A("pat", 0, 16), A("ea"), A("eb"), ALU.add)
-    tt(A("pat", 16, 32), A("ea"), A("eb"), ALU.add)
-    ts(A("l8"), A("l2"), 448.0, ALU.add)
-    for t in range(2):
-        ts(A("hl", 28 * t, 28 * t + 28), A("hti", 0, 28), 4.0, ALU.mult, float(t), ALU.add)
-    copy(A("db"), A("pat", 0, 16, by=A("lw")), "s")
-    ts(column(2), A("pat", 15, 16), -2 * BIG, ALU.add)
-    ts(A("pat", 31, 32), A("pat", 15, 16), -2 * BIG, ALU.add)
-    quant(A("qu"), A("qus"), A("ut"))
-    for t in range(2, 4):
-        ts(A("hl", 28 * t, 28 * t + 28), A("hti", 0, 28), 4.0, ALU.mult, float(t), ALU.add)
-    fill(A("pat", 16, 32, p=g0), 0.0)
-    ts(A("kc"), A("kk"), MID, ALU.add)
-    ul = A("ul")
-    copy(A("qps"), A("qus", by=ul), "s")
-    copy(A("qp", cast=dt.uint32), A("qu", cast=dt.uint32, by=ul))
-    fill(A("pat", 16, 17, p=g0), 16.0)
-    for r in range(4):
-        q = (r - 1) % 4
-        copy(A("hu", 28, 56, p=(32 * r, 32 * r + 32)), A("hti", 0, 28, p=(32 * q, 32 * q + 32)))
-    for t in range(4):
-        copy(A("ec", 513 * t, 512 * t + 512, 4), A("eye"), "s")
-    copy(A("dw"), A("pat", 16, 32, by=A("lw")), "s")
+    def unit(t):
+        quant(A("qe", 128 * t, 128 * t + 128), A("qes", 128 * t, 128 * t + 128), A("ec", 3 - t, 515 - t))
 
-    def scores(s, c, w):
+    def scores(s, c, sides):
         a, b = CH[c]
-        mm(score(2 * c + w, b - a), A("qp", 128 * w, 128 * w + 128), A("qps", 128 * w, 128 * w + 128),
-           A("qx%d" % s, a, b), A("qxs%d" % s, a, b))
+        for w in sides:
+            mm(score(2 * c + w, b - a), A("qp", 16 - 16 * w, 144 - 16 * w), A("qps", 16 - 16 * w, 144 - 16 * w),
+               A("qx%d" % s, a, b), A("qxs%d" % s, a, b))
 
-    def settle(s, c, sides=(1, 0)):
+    def settle(s, c, sides=()):
         a, b = CH[c]
         q, sc = A("qx%d" % s, a, b), A("qxs%d" % s, a, b)
         quant(q, sc, A("x%d" % s, 4 * a, 4 * b))
         if s < 3:
-            for w in sides:
-                scores(s, c, w)
+            scores(s, c, sides)
         else:
             mm(score(c, b - a), A("qv"), A("qvs"), q, sc)
-            if c != 1:
-                a = CH[c // 2][0]
-                dma("y", ext(T.oc[:, 4 * a:4 * b]), A("qx3", a, b, cast=dt.uint8), "oo")
 
-    def signs(c, w, q):
+    def signs(w, c, q):
         a, b = CH[c]
         out = A(("bt", "bl")[w], a, b)
         if q == "s":
@@ -291,191 +281,266 @@ def rank_program(g, core, T, topo):
         else:
             ts(out, score(2 * c + w, b - a), 0.0, ALU.is_gt)
 
-    def host(s, c, who, src):
+    def host(s, c, who, src="x"):
         a, b = CHH[s][c]
         for t in range(4):
-            if who[t] != "-":
-                out, win = A("h%d" % s, 4 * a + t, 4 * b, 4), A(src, by=A("hl", 28 * t + a // 16, 28 * t + b // 16))
-                if src[0] == "k":
-                    act(out, win, scale=2.0 ** -6)
-                else:
-                    copy(out, win, who[t])
+            out, win = A("h%d" % s, 4 * a + t, 4 * b, 4), A("%s%d" % (src, s - 1), by=A("hl", 28 * t + a // 16, 28 * t + b // 16))
+            if who[t] == "-":
+                continue
+            if src == "k":
+                times(out, win, 2.0 ** -6, who[t])
+            else:
+                copy(out, win, who[t])
 
-    settle(0, 0)
-    settle(0, 1)
-    ts(A("db", 15, 448, 16), A("i32"), column(2), ALU.add)
-    settle(0, 2)
-    host(1, 0, "ss--", "x0")
-    for c in range(2):
-        signs(c, 1, "v")
-        signs(c, 0, "v")
-    copy(A("hu", 0, 28), A("hti", 28, 56))
+    def codes(s, c, planes=True):
+        a, b, k = CHH[s][c] + ("%d" % s,)
+        quant(A("qh" + k, a, b), A("qhs" + k, a, b), A("h" + k, 4 * a, 4 * b))
+        send(s, A("hc" + k, a, b, cast=dt.uint8), A("qh" + k, a, b, cast=dt.uint8), "c%d%d" % (s, c))
+        if planes:
+            scales(s, c)
 
-    for s in STEPS:
-        k = "%d" % s
-        xo, xn, ko, kn = "x%d" % (s - 1), "x" + k, "k%d" % (s - 1), "k" + k
-        first = s == 1
-        ini = A("ini", 0, 1)
+    def scales(s, c):
+        a, b, k = CHH[s][c] + ("%d" % s,)
+        send(s, A("hcs" + k, a, b), A("qhs" + k, a, b), "c%d%d" % (s, c))
 
-        def codes(c):
+    def list_side(s):
+        tt(A("ib", 56 * s - 55, 56 * s, 2), wrapped("sl"), A("kk"), ALU.add)
+        send(s, A("br%d" % s), A("ib", 56 * s - 56, 56 * s), "k%d" % s)
+
+    def table_side(s):
+        ts(A("it%d" % s), wrapped("st"), column(0), ALU.add)
+        send(s, A("ir%d" % s), A("it%d" % s), "j%d" % s)
+
+    def unpack(s, c):
+        a, b, k = CHH[s][c] + ("%d" % s,)
+        for t in range(4):
+            mm(bank(c, t, b - a), A("qe", 128 * t, 128 * t + 128), A("qes", 128 * t, 128 * t + 128), A("hc" + k, a, b), A("hcs" + k, a, b))
+
+    def grown(i):
+        act(A("k0", 448 * i, 448 * i + 448), A("x0", 448 * i, 448 * i + 448), scale=64.0)
+
+    def walk(s):
+        first, last = s == 1, s == 3
+        pieces = [(c, t) for c in range(3) for t in range(4)]
+
+        def larger():
+            c, t = pieces.pop(0)
             a, b = CHH[s][c]
-            quant(A("qh" + k, a, b), A("qhs" + k, a, b), A("h" + k, 4 * a, 4 * b))
-            send(s, A("hc" + k, a, b, cast=dt.uint8), A("qh" + k, a, b, cast=dt.uint8), "c%d%d" % (s, c))
+            tt(A("m%d" % s, 448 * t + a, 448 * t + b), A("x%d" % (s - 1), 4 * a + t, 4 * b, 4), bank(c, t, b - a), ALU.max)
 
-        def scales(c):
-            a, b = CHH[s][c]
-            send(s, A("hcs" + k, a, b), A("qhs" + k, a, b), "c%d%d" % (s, c))
-
-        def unpack(c):
-            a, b = CHH[s][c]
-            for t in range(4):
-                mm(bank(c, t, b - a), A("qe", 128 * t, 128 * t + 128), A("qes", 128 * t, 128 * t + 128), A("hc" + k, a, b), A("hcs" + k, a, b))
-
-        def larger(c, t):
-            a, b = CHH[s][c]
-            tt(A("m" + k, 448 * t + a, 448 * t + b), A(xo, 4 * a + t, 4 * b, 4), bank(c, t, b - a), ALU.max)
-
-        signs(2, 1, "v")
         if first:
-            signs(2, 0, "s")
-            for r in range(1, 4):
-                copy(A("glu", 56, 112, p=(32 * r, 32 * r + 32)), A("gli", 56, 112, p=(32 * r - 32, 32 * r)))
-            copy(A("glu", 56, 112, p=g0), A("gli", 56, 112, p=(96, 112)))
+            scan(A("la"), A("br1"), A("dc"), 0.0, ALU.mult)
+            unpack(s, 0)
+            shared("t0", "gt", "ir1", 14)
+            copy(A("l1"), A("la", 1, 56, 2))
+            codes(1, 2)
+            iota(A("p2", 448, 896), [[0, 448]], 0)
+            shared("p1", "t0", "l1", 16)
+            grown(1)
+            grown(0)
         else:
-            signs(1, 0, "s")
-            signs(2, 0, "v")
-            codes(0)
-        shared("al", 0, ("bl", 0, 448), "hu", 14 if first else 10, True, 28)
-        shared("at", 0, ("bt", 0, 448), "hu", 14, True)
+            larger()
+            larger()
+            scan(A("la"), A("br%d" % s), A("dc"), 0.0, ALU.mult)
+            shared("t0", "gt", "ir%d" % s, 14)
+            copy(A("l1"), A("la", 1, 56, 2))
+            larger()
+            shared("p1", "t0", "l1", 16)
+        larger()
+        scan(A("s1"), A("p1"), A("dw"), ini)
+        if first:
+            larger()
+        ts(A("l2", p=(32, 64)), wrapped("s1", (0, 32)), column(1, (0, 32)), ALU.add)
+        for a in (64, 96):
+            ts(A("l2", p=(a, a + 32)), wrapped("s1", (a - 32, a)), BIG + MID, ALU.add)
+        if last:
+            ts(A("l2", p=g0), wrapped("s1", (96, 112)), BIG + MID, ALU.add)
+        if first:
+            larger()
+            larger()
+        unpack(s, 1)
+        if not first:
+            larger()
+        shared("p2", "p1", "l2", 16 if first else 14)
+        if first:
+            copy(A("dz"), A("pat", 0, 16, by=A("lw", 0, 14)), "s")
+        if not last:
+            copy(A("p2", 448, 896, p=low), A("p2", 0, 448, p=high), "s")
+        larger()
+        scan(A("s2"), A("p2", 0, 448), A("dw"), ini)
+        larger()
+        if last:
+            ts(A("l3", p=high), wrapped("s2", low), column(1, low), ALU.add)
+            ts(A("l3", p=g0), wrapped("s2", (64, 80)), BIG + MID, ALU.add)
+            larger()
+            unpack(s, 2)
+            shared("p3", "p2", "l3", 16)
+            act(A("p8"), A("p3"), ACT.Identity, bias=MID)
+            dma("y", ext(T.pl[0:7, :]), (T.p8[16:128:16, :], A("p8")[1]), "op_")
+            dma("y", ext(T.pl[7:8, :]), A("p8", p=(0, 1)), "op_")
+            larger()
+            scan(A("s3"), A("p3"), A("dw"), ini)
+            larger()
+            ts(A("vl"), wrapped("s3"), column(1), ALU.add)
+        else:
+            ts(A("l4", p=high), wrapped("s2", low, 0, 224), column(1, low), ALU.add)
+            ts(A("l4", p=low), wrapped("s2", low, 224, 448), column(1, low), ALU.add, 448.0, ALU.add)
+            ts(A("vl", p=low), wrapped("s2", low), column(1, low), ALU.add)
+            larger()
+            copy(A("p3", 0, 128), A("p2", by=A("l4", 0, 8)))
+            copy(A("p3", 128, 224), A("p2", by=A("l4", 8, 14)), "s")
+            if first:
+                grown(2)
+                grown(3)
+                larger()
+            unpack(s, 2)
+            if not first:
+                larger()
+            scan(A("s3", 0, 224), A("p3", 0, 224), A("dz"))
+            larger()
+            ts(A("vl", 0, 14, p=high), wrapped("s3", high, 0, 224), BIG + MID, ALU.add)
+            ts(A("vl", 14, 28, p=high), wrapped("s3", low, 0, 224), BIG + MID, ALU.add)
+        while pieces:
+            larger()
+
+    def mosaic(s, c, who):
+        a, b = CH[c]
+        for t in range(4):
+            if who[t] != "-":
+                copy(A("z%d" % s, 4 * a + t, 4 * b, 4), A("m%d" % s, 448 * t, 448 * t + 448, by=A("vl", a // 16, b // 16)), who[t])
+
+    def layer(s, c):
+        a, b, k = CH[c] + ("%d" % s,)
+        quant(A("qz" + k, a, b), A("qzs" + k, a, b), A("z" + k, 4 * a, 4 * b))
+        for t in range(4):
+            mm(bank(c, t, b - a), A("qw", 128 * t, 128 * t + 128), A("qws", 128 * t, 128 * t + 128), A("qz" + k, a, b), A("qzs" + k, a, b))
+
+    def finish(s, c):
+        a, b = CH[c]
+        for t in range(4):
+            tt(A("k%d" % s, 4 * a + t, 4 * b, 4), bank(c, t, b - a), A("k%d" % (s - 1), 4 * a + t, 4 * b, 4), ALU.add)
+
+    def shrink(s, a, b, q):
+        times(A("x%d" % s, 4 * a, 4 * b), A("k%d" % s, 4 * a, 4 * b), 2.0 ** -6, q)
+
+    def state(s):
+        mosaic(s, 0, "svsv")
+        mosaic(s, 1, "ssv-")
+        layer(s, 0)
+        mosaic(s, 2, "ssss")
+        mosaic(s, 1, "---v")
+        layer(s, 1)
+        finish(s, 0)
+        layer(s, 2)
+        shrink(s, 0, 160, "s")
+        finish(s, 1)
+        shrink(s, 160, 240, "s")
+        finish(s, 2)
+
+    def result(c, q):
+        a, b = CH[c]
+        copy(A("yb", a, b), score(c, b - a), q)
+
+    def store(c, d):
+        a, b = CH[c][0], CH[d][1]
+        dma("y", ext(T.oc[:, 4 * a:4 * b]), A("qx3", a, b, cast=dt.uint8), "oo")
+
+    host(1, 0, "ss--")
+    settle(0, 0, (1, 0))
+    host(1, 0, "--vv")
+    settle(0, 1, (1, 0))
+    settle(0, 2, (1, 0))
+    codes(1, 0, False)
+    copy(A("dw"), A("pat", 16, 32, by=A("lw")), "s")
+    last_places = A("db", 15, 448, 16)
+    run("s", lambda: g.scalar.activation(last_places[0], T.i32[:, :], ACT.Identity, bias=T.pat[:, 15:16]), [last_places], [A("i32"), A("pat", 15, 16)])
+    signs(0, 0, "s")
+    signs(1, 0, "v")
+    signs(1, 1, "v")
+    copy(A("hu"), A("hti", 28, 84))
+    signs(0, 2, "s")
+    signs(1, 2, "v")
+    signs(0, 1, "v")
+    shared("al", "bl", "hu", 14, True, 28)
+    shared("at", "bt", "hu", 12, True)
+    copy(A("glu"), A("gli", 56, 112))
+    host(1, 1, "s--s")
+    host(1, 2, "-s--")
+    copy(A("gt", 0, 448), A("idb", by=A("glu", 0, 28)), "s")
+    scan(A("sl"), A("al"), A("db"))
+    scan(A("st"), A("at"), A("db"))
+    list_side(1)
+    for i in range(2):
+        copy(A("g1", 32 * i, 32 * i + 32), A("gli", i, 64, 2))
+    table_side(1)
+    scales(1, 0)
+    turn(A("g2"), A("g1"))
+    ts(A("shl"), A("sh"), A("nt", 64, 65), ALU.add)
+    copy(A("g3"), A("g2", by=A("shl")), "s")
+    copy(A("gt", 448, 896), A("idb", by=A("glu", 28, 56)), "s")
+    host(1, 1, "-vv-")
+    unit(0)
+    codes(1, 1)
+    turn(A("g4"), A("g3"))
+    unit(1)
+    host(1, 2, "v---")
+    tt(A("dc", 0, 56, 2), A("g4", 32, 60), A("g4", 0, 28), ALU.subtract)
+    copy(A("dc", 1, 56, 2), A("g4", 0, 28), "s")
+    host(1, 2, "--sv")
+    unit(2)
+    unit(3)
+    walk(1)
+    waits("y", A("hc1")[1], [])
+    dma("y", A("vt"), ext(T.v[:, :]), "dv")
+
+    for s in (2, 3):
+        state(s - 1)
+        host(s, 0, "sss-", "k")
+        settle(s - 1, 0, (1, 0))
+        shrink(s - 1, 240, 320, "v")
+        shrink(s - 1, 320, 448, "v")
+        settle(s - 1, 1, (1,))
+        settle(s - 1, 2, (1,))
+        signs(1, 0, "s")
+        host(s, 0, "---v", "k")
+        scores(s - 1, 2, (0,))
+        scores(s - 1, 1, (0,))
+        signs(0, 0, "v")
+        codes(s, 0)
+        for w, c, q in ((1, 2, "v"), (1, 1, "s"), (0, 2, "s"), (0, 1, "v")):
+            signs(w, c, q)
+        shared("al", "bl", "hu", 16, True, 28)
+        shared("at", "bt", "hu", 14, True)
+        host(s, 1, "sss-")
         scan(A("sl"), A("al"), A("db"))
         scan(A("st"), A("at"), A("db"))
-        tt(A("ib" + k), wrapped("sl"), A("kk"), ALU.add)
-        send(s, A("br" + k), A("ib" + k), "k" + k)
-        if first:
-            copy(A("glu", 0, 56), A("gli", 0, 56))
-        ts(A("it" + k), wrapped("st"), column(0), ALU.add)
-        send(s, A("ir" + k), A("it" + k), "j" + k)
-        if first:
-            host(s, 0, "--sv", xo)
-            host(s, 1, "---v", xo)
-            codes(0)
-        scales(0)
-        host(s, 1, "sss-" if first else "ssvv", xo)
-        codes(1)
-        scales(1)
-        if first:
-            shared("gn", 0, ("idb", 0, 448), "glu", 20, False, 56, 56)
-            shared("gt", 0, ("idb", 0, 448), "glu", 12, False, 0, 56)
-            scan(A("s1"), A("gn", 0, 896, 2), A("db"))
-            scan(A("s2"), A("gn", 1, 896, 2), A("db"))
-            for a in (0, 256):
-                spare.append(lambda a=a: quant(A("qe", a, a + 256), A("qes", a, a + 256), A("ec", 4 * a, 4 * a + 1024)))
-            for a in (0, 448):
-                spare.append(lambda a=a: ts(A(ko, a, a + 448), A(xo, a, a + 448), 64.0, ALU.mult))
-            gap()
-            tt(A("dl"), wrapped("s2"), wrapped("s1"), ALU.subtract)
-            tt(A("cl"), wrapped("s1"), A("kc"), ALU.add)
-            waits("y", A("hc1")[1], [])
-            dma("y", A("vt"), ext(T.v[:, :]), "dv")
-        if s == 3:
-            quant(A("qv"), A("qvs"), A("vt"))
-        tt(A("la"), A("br" + k), A("dl"), ALU.mult)
-        gap()
-        tt(A("lb"), A("la"), A("cl"), ALU.add)
-        shared("t0", 0, ("gt", 0, 896), "ir" + k, 12)
-        copy(A("l1"), A("lb"))
-        gap()
-        shared("pw", 0, ("t0", 0, 448), "l1", 14)
-        if first:
-            act(A(ko, 896, 1792), A(xo, 896, 1792), scale=64.0)
-        gap()
-        scan(A("s1"), A("pw", 0, 448), A("dw"), ini)
-        unpack(0)
-        unpack(1)
-        for c in range(2):
-            for t in range(4):
-                spare.append(lambda c=c, t=t: larger(c, t))
-        early = int(not first)
-        gap(early)
-        ts(A("l2", p=(32, 64)), wrapped("s1", (0, 32)), column(1, (0, 32)), ALU.add)
-        ts(A("l2", p=(96, 128)), wrapped("s1", (64, 96)), BIG + MID, ALU.add)
-        gap(early)
-        shared("p2", 0, ("pw", 0, 448), "l2", 14)
-        gap()
-        scan(A("s2"), A("p2"), A("dw"), ini)
-        gap(1 - early)
-        ts(A("l3", p=(64, 96)), wrapped("s2", (32, 64)), BIG + MID, ALU.add)
-        ts(A("l3", p=(96, 128)), wrapped("s2", (32, 64)), BIG + MID, ALU.add)
-        gap()
-        shared("pw", 448, ("p2", 0, 448), "l3", 14)
-        gap()
-        scan(A("s3"), A("pw", 448, 896), A("dw"), ini)
-        gap()
-        ts(A("vl"), wrapped("s3"), column(1), ALU.add)
-        gap(len(spare))
-
-        def mosaic(c, who):
-            a, b = CH[c]
-            for t in range(4):
-                if who[t] != "-":
-                    copy(A("z" + k, 4 * a + t, 4 * b, 4), A("m" + k, 448 * t, 448 * t + 448, by=A("vl", a // 16, b // 16)), who[t])
-
-        def layer(c):
-            a, b = CH[c]
-            quant(A("qz" + k, a, b), A("qzs" + k, a, b), A("z" + k, 4 * a, 4 * b))
-            for t in range(4):
-                mm(bank(c, t, b - a), A("qw", 128 * t, 128 * t + 128), A("qws", 128 * t, 128 * t + 128),
-                   A("qz" + k, a, b), A("qzs" + k, a, b))
-
-        def finish(c):
-            a, b = CH[c]
-            for t in range(4):
-                tt(A(kn, 4 * a + t, 4 * b, 4), bank(c, t, b - a), A(ko, 4 * a + t, 4 * b, 4), ALU.add)
-
-        def shrink(c, q):
-            a, b = CH[c]
-            if q == "v":
-                ts(A(xn, 4 * a, 4 * b), A(kn, 4 * a, 4 * b), 2.0 ** -6, ALU.mult)
-            else:
-                for t in range(4):
-                    act(A(xn, 4 * a + t, 4 * b, 4), A(kn, 4 * a + t, 4 * b, 4), scale=2.0 ** -6)
-
-        mosaic(0, "ssvs")
-        mosaic(1, "--vv")
-        layer(0)
-        mosaic(1, "ss--")
-        mosaic(2, "sssv")
-        if s == 3:
-            copy(A("l8", p=g0), A("vl", p=(96, 112)))
-        layer(1)
-        finish(0)
-        layer(2)
-        shrink(0, "s")
-        finish(1)
-        shrink(1, "s")
-        finish(2)
-        settle(s, 0)
-        if s < 3:
-            host(s + 1, 0, "ssss", kn)
+        unpack(s, 0)
+        list_side(s)
+        host(s, 1, "---v")
+        table_side(s)
+        codes(s, 1)
+        host(s, 2, "svss")
+        codes(s, 2)
+        if s == 2:
+            ts(A("l3"), A("i8", 0, 28), 2.0, ALU.mult, i1, ALU.add)
         else:
-            act(A("p8"), A("pw", by=A("l8")), ACT.Identity, bias=MID)
-            dma("s", ext(T.pl[0:7, :]), (T.p8[16:128:16, :], A("p8")[1]), "op_")
-            dma("s", ext(T.pl[7:8, :]), A("p8", p=(0, 1)), "op_")
-        shrink(2, "v")
-        settle(s, 1, (1,))
-        settle(s, 2, (1,))
-        if s < 3:
-            scores(s, 1, 0)
-            scores(s, 2, 0)
-            signs(0, 1, "v")
-            signs(0, 0, "v")
-            signs(1, 1, "v")
+            quant(A("qv"), A("qvs"), A("vt"))
+        walk(s)
 
-    for c, (a, b) in enumerate(CH):
-        copy(A("yb", a, b), score(c, b - a))
-    dma("y", ext(T.y[:, :]), A("yb"), "oy")
+    state(3)
+    shrink(3, 240, 320, "v")
+    settle(3, 0)
+    store(0, 0)
+    shrink(3, 320, 448, "v")
+    result(0, "s")
+    settle(3, 1)
+    settle(3, 2)
+    store(1, 2)
+    result(1, "v")
     for i in range(4):
         dma("s", ext(T.osc[4 * i:4 * i + 4, :]), A("qxs3", p=(32 * i, 32 * i + 4)), "os_")
+    result(2, "v")
+    dma("y", ext(T.y[:, :]), A("yb"), "oy")
     for sem in sorted(total):
         if max(seen[q].get(sem, 0) for q in queue) < total[sem]:
-            queue[{"oo": "y", "oy": "y", "op_": "s", "os_": "s"}.get(sem, "p")].wait_ge(T.sem[sem], total[sem])
+            queue[{"oo": "y", "oy": "y", "op_": "y", "os_": "s"}.get(sem, "p")].wait_ge(T.sem[sem], total[sem])

from concourse.bass import DstId, RemoteDMATransfer
from concourse.mybir import dt, AluOpType, ActivationFunctionType

C = 448
STEPS = (1, 2, 3)
CH = ((0, 160), (160, 320), (320, 448))
CHL = ((0, 320), (320, 448))
CHH = dict((_s, ((0, 128), (128, 288), (288, 448))) for _s in STEPS)
BIG = 512.0
MID = 224.0
TOP = 240.0
ALU = AluOpType
ACT = ActivationFunctionType
F8, U8, BF, F32, I32, U16, F16 = "float8_e4m3fn_x4", "uint8", "bfloat16", "float32", "int32", "uint16", "float16"

SCRATCH = {"pa": ("psum", [128, 2048], F32), "pb": ("psum", [128, 2048], F32)}


def _sbuf(kind, **widths):
    for name in widths:
        SCRATCH[name] = ("sbuf", [128, widths[name]], kind)


_sbuf(I32, gli=112, hti=84, uli=9)
_sbuf(U16, glu=56, shl=4, hu=56, hl=112, ul=9, lw=28, l1=28, l2=28, l3=28, l4=14, vl=28)
_sbuf(BF, ut=512, vt=512, ec=516, one=128, pat=32, ini=2, ib=168, idb=448, db=448, dw=448, dz=224, gt=896, bt=448, bl=448,
      at=448, al=448, t0=448, p1=448, p2=896, p3=448)
_sbuf(F16, st=448, sl=448, s1=448, s2=448, s3=448)
_sbuf(F8, qu=128, qp=144, qv=128, qe=512, qw=512)
_sbuf(U8, qus=128, qps=144, qvs=128, qes=512, qws=512)
_sbuf(F32, col=2, sh=4, nn=96, nt=96, e=32, ea=32, eb=32, i8=56, i32=28, kk=28, g1=64, g2=64, g3=64, g4=64, dc=56, la=56,
      p8=448, yb=448)
for _k in range(4):
    for _n, _w, _d in (("x", 1792, BF), ("k", 1792, BF), ("qx", 448, F8), ("qxs", 448, U8)):
        SCRATCH["%s%d" % (_n, _k)] = ("sbuf", [128, _w], _d)
for _k in STEPS:
    for _n, _w, _d in (("h", 1792, BF), ("m", 1792, BF), ("z", 1792, BF), ("qh", 448, F8), ("hc", 448, F8), ("qz", 448, F8),
                       ("qhs", 448, U8), ("hcs", 448, U8), ("qzs", 448, U8), ("it", 28, U16), ("ir", 28, U16), ("br", 56, BF)):
        SCRATCH["%s%d" % (_n, _k)] = ("sbuf", [128, _w], _d)
SEMAPHORES = ["v", "s", "t", "p", "rl", "dgl", "dg2", "dht", "dx0", "dx1", "dh2", "du", "dw", "dv", "oo", "os_", "oy", "op_"]
for _k in STEPS:
    SEMAPHORES += ["j%d" % _k, "k%d" % _k, "c%d0" % _k, "c%d1" % _k, "c%d2" % _k]


def rank_program(g, core, T, topo):
    rank = T.rank_of(core)
    if rank is None:
        return
    queue = {"v": g.vector, "s": g.scalar, "t": g.tensor, "p": g, "y": g.sync}
    total, log, known = {}, {}, {}
    seen = dict((q, {}) for q in queue)

    def A(name, a=0, b=None, step=1, p=None, cast=None, by=None):
        t = T[name]
        b = t.shape[1] if b is None else b
        lo, hi = p if p else (0, 128)
        reg = [(name, lo, hi, a, b, step)]
        if name in ("pa", "pb"):
            reg = [(name, 0, 128, a // 512 * 512, (b + 511) // 512 * 512, 1)]
        if p:
            v = t[lo:hi, a:b:step] if step > 1 else t[lo:hi, a:b]
        else:
            v = t[:, a:b:step] if step > 1 else t[:, a:b]
        if cast is not None:
            v = v.bitcast(cast)
        if by is not None:
            v = v.indirect(by[0])
            reg = reg + by[1]
        return v, reg

    def touch(r, s):
        apart = r[5] == s[5] and (r[3] - s[3]) % r[5] != 0
        return r[1] < s[2] and s[1] < r[2] and r[3] < s[4] and s[3] < r[4] and not apart

    def covers(r, s):
        same = r[5] == 1 or r[5] == s[5] and (r[3] - s[3]) % r[5] == 0
        return r[1] <= s[1] and s[2] <= r[2] and r[3] <= s[3] and s[4] <= r[4] and same

    def waits(q, reads, writes):
        need = {}
        for regs, wr in ((reads, False), (writes, True)):
            for r in regs:
                for reg, was, sem, val in log.get(r[0], []):
                    if touch(r, reg) and (wr or was or r[0] in ("pa", "pb")):
                        need[sem] = max(need.get(sem, 0), total[sem] if val is None else val)
        for sem in need:
            for other, val in known.get((sem, need[sem]), {}).items():
                if other != sem and seen[q].get(other, 0) < val:
                    seen[q][other] = val
        for sem in sorted(need):
            if seen[q].get(sem, 0) < need[sem]:
                queue[q].wait_ge(T.sem[sem], need[sem])
                seen[q][sem] = need[sem]

    def note(reads, writes, sem, val):
        for r in writes:
            log[r[0]] = [e for e in log.get(r[0], []) if not covers(r, e[0])] + [(r, True, sem, val)]
        for r in reads:
            log.setdefault(r[0], []).append((r, False, sem, val))

    def run(q, call, outs, ins):
        reads = [r for o in ins for r in o[1]]
        writes = [r for o in outs for r in o[1]]
        waits(q, reads, writes)
        call().then_inc(T.sem[q], 1)
        total[q] = total.get(q, 0) + 1
        note(reads, writes, q, total[q])
        known[(q, total[q])] = dict(seen[q])

    def dma(q, out, in_, sem):
        waits(q, in_[1], out[1])
        queue[q].dma_start(out[0], in_[0]).then_inc(T.sem[sem], 16)
        total[sem] = total.get(sem, 0) + 16
        note(in_[1], out[1], sem, None)

    def ext(view):
        return view, []

    def send(step, out, in_, sem):
        dst = T.cores[rank ^ step]
        rid, pid, _ = topo.addr(dst)
        waits("p", in_[1], [])
        g.remote_dma(out[0], in_[0], T.sem[sem], T.sem.rl, pid, rid, topo.mask(core, dst))
        total["rl"] = total.get("rl", 0) + len(topo.engines(core, dst))
        total[sem] = total.get(sem, 0) + len(topo.engines(dst, core))
        note([], out[1], sem, None)

    def act(out, in_, func=ACT.Copy, **kw):
        run("s", lambda: g.scalar.activation(out[0], in_[0], func, **kw), [out], [in_])

    def copy(out, in_, q="v"):
        if q == "v":
            run("v", lambda: g.vector.tensor_copy(out[0], in_[0]), [out], [in_])
        else:
            act(out, in_)

    def ts(out, in_, a, op0, b=None, op1=None):
        col = [c for c in (a, b) if isinstance(c, tuple)]
        a0, b0 = [c[0] if isinstance(c, tuple) else c for c in (a, b)]
        if op1 is None:
            run("v", lambda: g.vector.tensor_scalar(out[0], in_[0], a0, None, op0), [out], [in_] + col)
        else:
            run("v", lambda: g.vector.tensor_scalar(out[0], in_[0], a0, b0, op0, op1), [out], [in_] + col)

    def times(out, in_, c, q):
        if q == "v":
            ts(out, in_, c, ALU.mult)
        else:
            act(out, in_, scale=c)

    def tt(out, a, b, op):
        run("v", lambda: g.vector.tensor_tensor(out[0], a[0], b[0], op), [out], [a, b])

    def fill(out, c):
        run("v", lambda: g.vector.memset(out[0], c), [out], [])

    def turn(out, in_):
        run("v", lambda: g.vector.transpose(out[0], in_[0]), [out], [in_])

    def quant(q, s, in_):
        run("v", lambda: g.vector.quantize_mx(q[0], s[0], in_[0]), [q, s], [in_])

    def mm(out, l, ls, r, rs):
        run("t", lambda: g.tensor.matmul_mx(out[0], l[0], ls[0], r[0], rs[0], True, True), [out], [l, ls, r, rs])

    def iota(out, pattern, base, f=True):
        if f:
            run("p", lambda: g.iota(out[0], pattern, base, 0, allow_small_or_imprecise_dtypes=True), [out], [])
        else:
            run("p", lambda: g.iota(out[0], pattern, base, 0), [out], [])

    def scan(out, in_, d, first=-BIG, op=ALU.max):
        col = [first] if isinstance(first, tuple) else []
        f0 = first[0] if col else first
        run("v", lambda: g.vector.tensor_tensor_scan(out[0], in_[0], d[0], f0, op, ALU.add), [out], [in_, d] + col)

    def wrapped(name, p=None, a=0, b=448):
        return A(name, a + 15, b, 16, p)

    def column(i, p=None):
        return A("col", i, i + 1, p=p)

    def bank(c, t, n):
        return A(("pa", "pb")[c % 2], 512 * t, 512 * t + n)

    def score(i, n):
        return A(("pb", "pa")[i // 4], 512 * (i % 4), 512 * (i % 4) + n)

    def shared(out, win, lst, cut, relu=False, base=0):
        for q, i, j in (("v", 0, cut), ("s", cut, 28)):
            o, w = A(out, 16 * i, 16 * j), A(win, 0, 896 if win == "gt" else 448, by=A(lst, base + i, base + j))
            if not relu:
                copy(o, w, q)
            elif q == "v":
                ts(o, w, 0.0, ALU.max)
            else:
                act(o, w, ACT.Relu)

    def turned(name, a, w, src, n, sem):
        dma("y", A(name, a, a + w, p=(n, 128)), ext(src[0:128 - n, :]), sem)
        dma("y", A(name, a, a + w, p=(0, n)), ext(src[128 - n:128, :]), sem)

    g0, low, high = (0, 16), (0, 64), (64, 128)
    dma("y", A("ut"), ext(T.u[:, :]), "du")
    dma("s", A("hti", 0, 28), ext(T.ht[:, :]), "dht")
    for c, (a, b) in enumerate(CHL):
        dma("sy"[c], A("x0", 4 * a, 4 * b), ext(T.x[:, 4 * a:4 * b]), "dx%d" % c)
    turned("gli", 56, 56, T.gl, 16, "dgl")
    turned("hti", 56, 28, T.ht, 32, "dh2")
    turned("hti", 28, 28, T.ht, 16, "dh2")

    iota(A("nn", 0, 32), [[0, 2], [1, 16]], 0)
    iota(A("nn", 32, 64), [[0, 2], [1, 8], [0, 2]], 0)
    iota(A("uli", 0, 2), [[16, 2]], 96, False)
    iota(A("uli", 2, 9), [[16, 7]], 0, False)
    iota(A("i8"), [[8, 56]], 0)
    fill(A("ec"), 0.0)
    fill(A("one"), 1.0)
    turn(A("nt", 0, 32), A("nn", 0, 32))
    i1 = A("nt", 0, 1)
    fill(column(1), BIG + MID)
    fill(A("ini"), -BIG)
    tt(A("e"), A("nn", 0, 32), A("nt", 0, 32), ALU.subtract)
    act(column(0), i1, ACT.Identity, scale=2.0, bias=3 * BIG)
    act(A("ini", 0, 1, p=g0), A("nt", 0, 1, p=g0), ACT.Identity, bias=TOP - 16)
    act(column(1, g0), A("nn", 0, 1, p=g0), ACT.Identity, bias=-TOP)
    fill(A("ib"), 0.0)
    ts(A("eb"), A("e"), 0.0, ALU.is_lt, -BIG, ALU.mult)
    ts(A("ea"), A("e"), 0.0, ALU.is_equal, BIG, ALU.mult)
    eye = A("ec", 3, 515, 4)
    run("p", lambda: g.affine_select(eye[0], T.one[:, :], [[-1, 128]], ALU.is_equal, 0.0, 0, 1), [eye], [A("one")])
    iota(A("nn", 64, 96), [[0, 2], [32, 2], [2, 8]], 0)
    iota(A("i32"), [[32, 28]], -1024)
    iota(A("idb"), [[1, 448]], -224)
    iota(A("sh"), [[1, 2], [16, 2]], 0)
    iota(A("kk"), [[-32, 28]], 1536)
    copy(A("ul"), A("uli"))
    tt(A("pat"), A("ea"), A("eb"), ALU.add)
    ts(A("lw"), A("i8", 0, 28), 0.0, ALU.mult, i1, ALU.add)
    ts(A("l2"), A("i8", 0, 28), 2.0, ALU.mult, i1, ALU.add)
    ts(A("pat", 15, 32, 16), A("pat", 15, 32, 16), -2 * BIG, ALU.add)
    copy(A("db"), A("pat", 0, 16, by=A("lw")), "s")
    ini, ul = A("ini", 0, 1), A("ul")
    quant(A("qu"), A("qus"), A("ut"))
    copy(A("qps"), A("qus", by=ul), "s")
    for t in range(4):
        ts(A("hl", 28 * t, 28 * t + 28), A("hti", 0, 28), 4.0, ALU.mult, float(t), ALU.add)
    copy(A("qp", cast=dt.uint32), A("qu", cast=dt.uint32, by=ul))
    turn(A("nt", 32, 96), A("nn", 32, 96))
    ts(A("gli", 0, 56, p=(0, 32)), A("i8", p=(0, 32)), A("nt", 32, 33, p=(0, 32)), ALU.add)
    dma("y", A("gli", 0, 56, p=(32, 128)), ext(T.gl[0:96, :]), "dg2")
    dma("y", A("gli", 0, 56, p=g0), ext(T.gl[96:112, :]), "dg2")
    waits("y", A("x0")[1], [])
    dma("y", A("qws"), ext(T.ws[:, :]), "dw")
    dma("y", A("qw", cast=dt.uint8), ext(T.wc[:, :]), "dw")
    ts(A("pat", 16, 32, p=g0), A("nn", 0, 16, p=g0), 0.0, ALU.is_equal, 16.0, ALU.mult)

    def unit(t):
        quant(A("qe", 128 * t, 128 * t + 128), A("qes", 128 * t, 128 * t + 128), A("ec", 3 - t, 515 - t))

    def scores(s, c, sides):
        a, b = CH[c]
        for w in sides:
            mm(score(2 * c + w, b - a), A("qp", 16 - 16 * w, 144 - 16 * w), A("qps", 16 - 16 * w, 144 - 16 * w),
               A("qx%d" % s, a, b), A("qxs%d" % s, a, b))

    def settle(s, c, sides=()):
        a, b = CH[c]
        q, sc = A("qx%d" % s, a, b), A("qxs%d" % s, a, b)
        quant(q, sc, A("x%d" % s, 4 * a, 4 * b))
        if s < 3:
            scores(s, c, sides)
        else:
            mm(score(c, b - a), A("qv"), A("qvs"), q, sc)

    def signs(w, c, q):
        a, b = CH[c]
        out = A(("bt", "bl")[w], a, b)
        if q == "s":
            act(out, score(2 * c + w, b - a), ACT.Sign)
        else:
            ts(out, score(2 * c + w, b - a), 0.0, ALU.is_gt)

    def host(s, c, who, src="x"):
        a, b = CHH[s][c]
        for t in range(4):
            out, win = A("h%d" % s, 4 * a + t, 4 * b, 4), A("%s%d" % (src, s - 1), by=A("hl", 28 * t + a // 16, 28 * t + b // 16))
            if who[t] == "-":
                continue
            if src == "k":
                times(out, win, 2.0 ** -6, who[t])
            else:
                copy(out, win, who[t])

    def codes(s, c, planes=True):
        a, b, k = CHH[s][c] + ("%d" % s,)
        quant(A("qh" + k, a, b), A("qhs" + k, a, b), A("h" + k, 4 * a, 4 * b))
        send(s, A("hc" + k, a, b, cast=dt.uint8), A("qh" + k, a, b, cast=dt.uint8), "c%d%d" % (s, c))
        if planes:
            scales(s, c)

    def scales(s, c):
        a, b, k = CHH[s][c] + ("%d" % s,)
        send(s, A("hcs" + k, a, b), A("qhs" + k, a, b), "c%d%d" % (s, c))

    def list_side(s):
        tt(A("ib", 56 * s - 55, 56 * s, 2), wrapped("sl"), A("kk"), ALU.add)
        send(s, A("br%d" % s), A("ib", 56 * s - 56, 56 * s), "k%d" % s)

    def table_side(s):
        ts(A("it%d" % s), wrapped("st"), column(0), ALU.add)
        send(s, A("ir%d" % s), A("it%d" % s), "j%d" % s)

    def unpack(s, c):
        a, b, k = CHH[s][c] + ("%d" % s,)
        for t in range(4):
            mm(bank(c, t, b - a), A("qe", 128 * t, 128 * t + 128), A("qes", 128 * t, 128 * t + 128), A("hc" + k, a, b), A("hcs" + k, a, b))

    def grown(i):
        act(A("k0", 448 * i, 448 * i + 448), A("x0", 448 * i, 448 * i + 448), scale=64.0)

    def walk(s):
        first, last = s == 1, s == 3
        pieces = [(c, t) for c in range(3) for t in range(4)]

        def larger():
            c, t = pieces.pop(0)
            a, b = CHH[s][c]
            tt(A("m%d" % s, 448 * t + a, 448 * t + b), A("x%d" % (s - 1), 4 * a + t, 4 * b, 4), bank(c, t, b - a), ALU.max)

        if first:
            scan(A("la"), A("br1"), A("dc"), 0.0, ALU.mult)
            unpack(s, 0)
            shared("t0", "gt", "ir1", 14)
            copy(A("l1"), A("la", 1, 56, 2))
            codes(1, 2)
            iota(A("p2", 448, 896), [[0, 448]], 0)
            shared("p1", "t0", "l1", 16)
            grown(1)
            grown(0)
        else:
            larger()
            larger()
            scan(A("la"), A("br%d" % s), A("dc"), 0.0, ALU.mult)
            shared("t0", "gt", "ir%d" % s, 14)
            copy(A("l1"), A("la", 1, 56, 2))
            larger()
            shared("p1", "t0", "l1", 16)
        larger()
        scan(A("s1"), A("p1"), A("dw"), ini)
        if first:
            larger()
        ts(A("l2", p=(32, 64)), wrapped("s1", (0, 32)), column(1, (0, 32)), ALU.add)
        for a in (64, 96):
            ts(A("l2", p=(a, a + 32)), wrapped("s1", (a - 32, a)), BIG + MID, ALU.add)
        if last:
            ts(A("l2", p=g0), wrapped("s1", (96, 112)), BIG + MID, ALU.add)
        if first:
            larger()
            larger()
        unpack(s, 1)
        if not first:
            larger()
        shared("p2", "p1", "l2", 16 if first else 14)
        if first:
            copy(A("dz"), A("pat", 0, 16, by=A("lw", 0, 14)), "s")
        if not last:
            copy(A("p2", 448, 896, p=low), A("p2", 0, 448, p=high), "s")
        larger()
        scan(A("s2"), A("p2", 0, 448), A("dw"), ini)
        larger()
        if last:
            ts(A("l3", p=high), wrapped("s2", low), column(1, low), ALU.add)
            ts(A("l3", p=g0), wrapped("s2", (64, 80)), BIG + MID, ALU.add)
            larger()
            unpack(s, 2)
            shared("p3", "p2", "l3", 16)
            act(A("p8"), A("p3"), ACT.Identity, bias=MID)
            dma("y", ext(T.pl[0:7, :]), (T.p8[16:128:16, :], A("p8")[1]), "op_")
            dma("y", ext(T.pl[7:8, :]), A("p8", p=(0, 1)), "op_")
            larger()
            scan(A("s3"), A("p3"), A("dw"), ini)
            larger()
            ts(A("vl"), wrapped("s3"), column(1), ALU.add)
        else:
            ts(A("l4", p=high), wrapped("s2", low, 0, 224), column(1, low), ALU.add)
            ts(A("l4", p=low), wrapped("s2", low, 224, 448), column(1, low), ALU.add, 448.0, ALU.add)
            ts(A("vl", p=low), wrapped("s2", low), column(1, low), ALU.add)
            larger()
            copy(A("p3", 0, 128), A("p2", by=A("l4", 0, 8)))
            copy(A("p3", 128, 224), A("p2", by=A("l4", 8, 14)), "s")
            if first:
                grown(2)
                grown(3)
                larger()
            unpack(s, 2)
            if not first:
                larger()
            scan(A("s3", 0, 224), A("p3", 0, 224), A("dz"))
            larger()
            ts(A("vl", 0, 14, p=high), wrapped("s3", high, 0, 224), BIG + MID, ALU.add)
            ts(A("vl", 14, 28, p=high), wrapped("s3", low, 0, 224), BIG + MID, ALU.add)
        while pieces:
            larger()

    def mosaic(s, c, who):
        a, b = CH[c]
        for t in range(4):
            if who[t] != "-":
                copy(A("z%d" % s, 4 * a + t, 4 * b, 4), A("m%d" % s, 448 * t, 448 * t + 448, by=A("vl", a // 16, b // 16)), who[t])

    def layer(s, c):
        a, b, k = CH[c] + ("%d" % s,)
        quant(A("qz" + k, a, b), A("qzs" + k, a, b), A("z" + k, 4 * a, 4 * b))
        for t in range(4):
            mm(bank(c, t, b - a), A("qw", 128 * t, 128 * t + 128), A("qws", 128 * t, 128 * t + 128), A("qz" + k, a, b), A("qzs" + k, a, b))

    def finish(s, c):
        a, b = CH[c]
        for t in range(4):
            tt(A("k%d" % s, 4 * a + t, 4 * b, 4), bank(c, t, b - a), A("k%d" % (s - 1), 4 * a + t, 4 * b, 4), ALU.add)

    def shrink(s, a, b, q):
        times(A("x%d" % s, 4 * a, 4 * b), A("k%d" % s, 4 * a, 4 * b), 2.0 ** -6, q)

    def state(s):
        mosaic(s, 0, "svsv")
        mosaic(s, 1, "ssv-")
        layer(s, 0)
        mosaic(s, 2, "ssss")
        mosaic(s, 1, "---v")
        layer(s, 1)
        finish(s, 0)
        layer(s, 2)
        shrink(s, 0, 160, "s")
        finish(s, 1)
        shrink(s, 160, 240, "s")
        finish(s, 2)

    def result(c, q):
        a, b = CH[c]
        copy(A("yb", a, b), score(c, b - a), q)

    def store(c, d):
        a, b = CH[c][0], CH[d][1]
        dma("y", ext(T.oc[:, 4 * a:4 * b]), A("qx3", a, b, cast=dt.uint8), "oo")

    host(1, 0, "ss--")
    settle(0, 0, (1, 0))
    host(1, 0, "--vv")
    settle(0, 1, (1, 0))
    settle(0, 2, (1, 0))
    codes(1, 0, False)
    copy(A("dw"), A("pat", 16, 32, by=A("lw")), "s")
    last_places = A("db", 15, 448, 16)
    run("s", lambda: g.scalar.activation(last_places[0], T.i32[:, :], ACT.Identity, bias=T.pat[:, 15:16]), [last_places], [A("i32"), A("pat", 15, 16)])
    signs(0, 0, "s")
    signs(1, 0, "v")
    signs(1, 1, "v")
    copy(A("hu"), A("hti", 28, 84))
    signs(0, 2, "s")
    signs(1, 2, "v")
    signs(0, 1, "v")
    shared("al", "bl", "hu", 14, True, 28)
    shared("at", "bt", "hu", 12, True)
    copy(A("glu"), A("gli", 56, 112))
    host(1, 1, "s--s")
    host(1, 2, "-s--")
    copy(A("gt", 0, 448), A("idb", by=A("glu", 0, 28)), "s")
    scan(A("sl"), A("al"), A("db"))
    scan(A("st"), A("at"), A("db"))
    list_side(1)
    for i in range(2):
        copy(A("g1", 32 * i, 32 * i + 32), A("gli", i, 64, 2))
    table_side(1)
    scales(1, 0)
    turn(A("g2"), A("g1"))
    ts(A("shl"), A("sh"), A("nt", 64, 65), ALU.add)
    copy(A("g3"), A("g2", by=A("shl")), "s")
    copy(A("gt", 448, 896), A("idb", by=A("glu", 28, 56)), "s")
    host(1, 1, "-vv-")
    unit(0)
    codes(1, 1)
    turn(A("g4"), A("g3"))
    unit(1)
    host(1, 2, "v---")
    tt(A("dc", 0, 56, 2), A("g4", 32, 60), A("g4", 0, 28), ALU.subtract)
    copy(A("dc", 1, 56, 2), A("g4", 0, 28), "s")
    host(1, 2, "--sv")
    unit(2)
    unit(3)
    walk(1)
    waits("y", A("hc1")[1], [])
    dma("y", A("vt"), ext(T.v[:, :]), "dv")

    for s in (2, 3):
        state(s - 1)
        host(s, 0, "sss-", "k")
        settle(s - 1, 0, (1, 0))
        shrink(s - 1, 240, 320, "v")
        shrink(s - 1, 320, 448, "v")
        settle(s - 1, 1, (1,))
        settle(s - 1, 2, (1,))
        signs(1, 0, "s")
        host(s, 0, "---v", "k")
        scores(s - 1, 2, (0,))
        scores(s - 1, 1, (0,))
        signs(0, 0, "v")
        codes(s, 0)
        for w, c, q in ((1, 2, "v"), (1, 1, "s"), (0, 2, "s"), (0, 1, "v")):
            signs(w, c, q)
        shared("al", "bl", "hu", 16, True, 28)
        shared("at", "bt", "hu", 14, True)
        host(s, 1, "sss-")
        scan(A("sl"), A("al"), A("db"))
        scan(A("st"), A("at"), A("db"))
        unpack(s, 0)
        list_side(s)
        host(s, 1, "---v")
        table_side(s)
        codes(s, 1)
        host(s, 2, "svss")
        codes(s, 2)
        if s == 2:
            ts(A("l3"), A("i8", 0, 28), 2.0, ALU.mult, i1, ALU.add)
        else:
            quant(A("qv"), A("qvs"), A("vt"))
        walk(s)

    state(3)
    shrink(3, 240, 320, "v")
    settle(3, 0)
    store(0, 0)
    shrink(3, 320, 448, "v")
    result(0, "s")
    settle(3, 1)
    settle(3, 2)
    store(1, 2)
    result(1, "v")
    for i in range(4):
        dma("s", ext(T.osc[4 * i:4 * i + 4, :]), A("qxs3", p=(32 * i, 32 * i + 4)), "os_")
    result(2, "v")
    dma("y", ext(T.y[:, :]), A("yb"), "oy")
    for sem in sorted(total):
        if max(seen[q].get(sem, 0) for q in queue) < total[sem]:
            queue[{"oo": "y", "oy": "y", "op_": "y", "os_": "s"}.get(sem, "p")].wait_ge(T.sem[sem], total[sem])
